import numpy as np
import ml_dtypes


def mxq(x, axis, fmt="e4m3"):
    dtype, down = {"e4m3": (ml_dtypes.float8_e4m3fn, 7), "e5m2": (ml_dtypes.float8_e5m2, 14)}[fmt]
    v = np.moveaxis(np.asarray(x, np.float32).astype(ml_dtypes.bfloat16).astype(np.float64), axis, -1)
    blocks = v.reshape(v.shape[:-1] + (-1, 32))
    amax = np.abs(blocks).max(-1, keepdims=True)
    byte = np.maximum(np.where(amax > 0, np.frexp(amax)[1] - 1 + 127, 0) - down, 1)
    scale = np.exp2(byte - 127.0)
    codes = (blocks / scale).astype(np.float32).astype(dtype).astype(np.float64)
    return np.moveaxis((codes * scale).reshape(v.shape), -1, axis)


WIDE = False


def mx_kscale(k):
    if not WIDE:
        return np.ones(k)
    levels = np.array([30, -30])
    if k % 512:
        return np.exp2(np.random.permutation(np.resize(levels, k // 32))).repeat(32)
    a = np.empty((k // 512, 16))
    for p in range(k // 512):
        a[p, :8] = np.random.permutation(np.resize(levels, 8))
        for g in range(8):
            far = levels[np.abs(levels - a[p, g]) >= 10]
            a[p, g + 8] = far[np.random.randint(len(far))]
    return np.exp2(a.ravel()).repeat(32)


BF16 = ml_dtypes.bfloat16


def bf(x):
    return np.asarray(x, np.float32).astype(BF16)


def f64(x):
    return np.asarray(x).astype(np.float64)


E2M1 = np.array([0.0, 0.5, 1.0, 1.5, 2.0, 3.0, 4.0, 6.0, -0.0, -0.5, -1.0, -1.5, -2.0, -3.0, -4.0, -6.0])


def pack_weight(w, fmt):
    k, n = w.shape
    w = f64(bf(w)).reshape(k // 32, 32, n)
    amax = np.abs(w).max(1)
    if fmt in ("e4m3", "e5m2"):
        byte = np.frexp(amax)[1] - 1 + 127 - (7 if fmt == "e4m3" else 14)
    else:
        mant, ex = np.frexp(amax / 6.0)
        byte = np.where(mant > 0.5, ex, ex - 1) + 127
    byte = np.clip(np.where(amax > 0, byte, 1), 1, 254)
    scaled = (w * np.exp2(127.0 - byte)[:, None, :]).reshape(k, n).astype(np.float32)
    by_word = np.ascontiguousarray(scaled.reshape(k // 512, 128, 4, n).transpose(0, 1, 3, 2))
    if fmt in ("e4m3", "e5m2"):
        words = by_word.astype(ml_dtypes.float8_e4m3fn if fmt == "e4m3" else ml_dtypes.float8_e5m2).view(np.uint8)
    else:
        c = by_word.astype(ml_dtypes.float4_e2m1fn).view(np.uint8) & 0xF
        words = c[..., 0::2] | (c[..., 1::2] << 4)
    return np.ascontiguousarray(words), np.ascontiguousarray(byte.astype(np.uint8).reshape(k // 512, 16, n))


def unpack_weight(words, scales, fmt):
    g, p, n, _ = words.shape
    if fmt in ("e4m3", "e5m2"):
        vals = np.ascontiguousarray(words).view(ml_dtypes.float8_e4m3fn if fmt == "e4m3" else ml_dtypes.float8_e5m2).astype(np.float64)
    else:
        nib = np.empty((g, p, n, 4), np.uint8)
        nib[..., 0::2] = words & 0xF
        nib[..., 1::2] = words >> 4
        vals = E2M1[nib]
    vals = vals * np.repeat(np.exp2(scales.astype(np.float64) - 127.0), 8, axis=1)[..., None]
    return vals.transpose(0, 1, 3, 2).reshape(g * 512, n)

def planes(Y):
    n, m = Y.shape
    b = f64(bf(Y)).reshape(n // 32, 32, m)
    amax = np.abs(b).max(1)
    byte = np.clip(np.where(amax > 0, np.frexp(amax)[1] - 1 + 127 - 7, 1), 1, 254)
    codes = (b * np.exp2(127.0 - byte)[:, None, :]).reshape(n, m).astype(np.float32).astype(ml_dtypes.float8_e4m3fn).view(np.uint8)
    words = codes.reshape(n // 512, 128, 4, m).transpose(0, 1, 3, 2)
    return np.ascontiguousarray(words), np.ascontiguousarray(byte.astype(np.uint8).reshape(n // 512, 16, m))


M, D, H = 1024, 1536, 1536


def setup_inputs():
    s = mx_kscale(D)
    vt = np.random.randn(D, M) * np.exp(np.random.randn(D, M))
    v_words, v_scales = pack_weight(vt * s[:, None], "e5m2")
    x = 0.7 * np.random.randn(M, D)
    spread = np.exp(0.6 * np.random.randn(H))
    w1 = np.random.randn(D, H) / np.sqrt(D) * spread[None, :]
    b1 = 0.5 * np.random.randn(H)
    db1 = 0.5 * np.random.randn(H)
    return {
        "v_words": v_words,
        "v_scales": v_scales,
        "x": bf(x * s[None, :]),
        "w1": bf(w1 / s[:, None]),
        "b1": bf(b1),
        "db1": bf(db1),
    }

def reference(v_words, v_scales, x, w1, b1, db1):
    vt = unpack_weight(v_words, v_scales, "e5m2")
    xq = mxq(f64(x), 1, "e4m3")
    wq = mxq(f64(w1), 0, "e4m3")
    z = (xq @ wq) + f64(b1)
    dz = (vt.T @ wq) + f64(db1)
    slope = 1.0 / (1.0 + np.exp(-z))
    y = slope * dz
    Y = y.T
    words, scales = planes(Y)
    return y, words, scales

@@ -1,0 +1,336 @@
+from contextlib import ExitStack
+
+import concourse.mybir as mybir
+from concourse.masks import make_identity
+
+M, D, H = 1024, 1536, 1536
+FLOPS = 2 * 2 * M * D * H
+
+F32 = mybir.dt.float32
+BF16 = mybir.dt.bfloat16
+I32 = mybir.dt.int32
+U32 = mybir.dt.uint32
+U8 = mybir.dt.uint8
+E4M3X4 = mybir.dt.float8_e4m3fn_x4
+E5M2X4 = mybir.dt.float8_e5m2_x4
+SIGMOID = mybir.ActivationFunctionType.Sigmoid
+ADD = mybir.AluOpType.add
+MULT = mybir.AluOpType.mult
+
+P = 128
+PACK = 4
+GROUP = P * PACK
+K_PASSES = D // GROUP
+H_GROUPS = H // GROUP
+HALF = 512
+HALVES = M // HALF
+PAIR = 256
+
+
+def tile_softplus_tangent_handoff_k2_kernel(tc, v_words, v_scales, x, w1, b1, db1, out_0, out_1, out_2):
+    nc = tc.nc
+    with ExitStack() as ctx:
+        keep = ctx.enter_context(tc.tile_pool(name="keep", bufs=1))
+        work = ctx.enter_context(tc.tile_pool(name="work", bufs=3))
+        psum = ctx.enter_context(tc.psum_pool(name="psum", bufs=1))
+        ctx.enter_context(tc.manual_schedule())
+
+        def bank(i):
+            return psum.tile([P, HALF], F32, name="bank%d" % i, tag="bank%d" % i)
+
+        ident = keep.tile([P, P], F32, name="ident")
+        v_plane = keep.tile([P, K_PASSES, M], U8, name="v_plane", align_bytes=64)
+        bias = keep.tile([P, H_GROUPS, PACK], BF16, name="bias")
+        dbias = keep.tile([P, H_GROUPS, PACK], BF16, name="dbias")
+        w_raw, w_codes, w_plane, v_codes, x_raw, x_codes, x_plane, y_plane = {}, {}, {}, {}, {}, {}, {}, {}
+        for g in range(K_PASSES):
+            for hg in range(H_GROUPS):
+                w_raw[g, hg] = keep.tile([P, PACK, GROUP], BF16, name="w_raw%d%d" % (g, hg))
+                w_codes[g, hg] = keep.tile([P, GROUP], U32, name="w_codes%d%d" % (g, hg), align_bytes=64)
+                w_plane[g, hg] = keep.tile([P, GROUP], U8, name="w_plane%d%d" % (g, hg), align_bytes=64)
+            for half in range(HALVES):
+                v_codes[g, half] = keep.tile([P, HALF], U32, name="v_codes%d%d" % (g, half), align_bytes=64)
+                x_codes[g, half] = keep.tile([P, HALF], U32, name="x_codes%d%d" % (g, half), align_bytes=64)
+                x_plane[g, half] = keep.tile([P, HALF], U8, name="x_plane%d%d" % (g, half), align_bytes=64)
+        for i in range(M // P):
+            x_raw[i] = keep.tile([P, D], BF16, name="x_raw%d" % i)
+        for hg in range(H_GROUPS):
+            y_plane[hg] = keep.tile([P, M], U8, name="y_plane%d" % hg, align_bytes=64)
+
+        def load_w(g, hg):
+            rows = w1[g * GROUP : (g + 1) * GROUP, hg * GROUP : (hg + 1) * GROUP]
+            nc.sync.dma_start(out=w_raw[g, hg][:], in_=rows.rearrange("(p j) c -> p j c", j=PACK))
+
+        def load_v(g, half):
+            words = v_words[g].rearrange("p n t -> p (n t)")[:, half * HALF * PACK : (half + 1) * HALF * PACK]
+            nc.sync.dma_start(out=v_codes[g, half][:].bitcast(I32), in_=words.bitcast(I32))
+
+        def load_x(pair):
+            for i in (2 * pair, 2 * pair + 1):
+                nc.sync.dma_start(out=x_raw[i][:], in_=x[i * P : (i + 1) * P, :])
+
+        def load_v_scales():
+            for q in range(4):
+                nc.sync.dma_start(
+                    out=v_plane[32 * q : 32 * q + 4, :, :].bitcast(I32),
+                    in_=v_scales[:, 4 * q : 4 * q + 4, :].rearrange("g r n -> r g n").bitcast(I32),
+                )
+
+        nc.vector.memset(v_plane[:].rearrange("p g n -> p (g n)").bitcast(I32), 0)
+        make_identity(nc, ident[:])
+        load_x(0)
+        load_w(0, 0)
+        load_x(1)
+        load_v(0, 0)
+        load_v_scales()
+        load_w(1, 0)
+        load_w(2, 0)
+        load_v(1, 0)
+        load_v(2, 0)
+        nc.sync.dma_start(out=bias[:], in_=b1.rearrange("(g p t) -> p g t", p=P, t=PACK))
+        nc.sync.dma_start(out=dbias[:], in_=db1.rearrange("(g p t) -> p g t", p=P, t=PACK))
+        load_x(2)
+        for g in range(K_PASSES):
+            load_v(g, 1)
+        load_x(3)
+        for hg in range(1, H_GROUPS):
+            for g in range(K_PASSES):
+                load_w(g, hg)
+
+        staged = {}
+
+        def sort_w(g, hg, part, engine):
+            grouped = work.tile([P, 2 * GROUP], BF16, name="w_grouped", tag="w_grouped", bufs=4, align_bytes=64)
+            src = w_raw[g, hg][:].rearrange("p j (m t) -> p t m j", t=PACK)[:, 2 * part : 2 * part + 2]
+            dst = grouped[:].rearrange("p (t m j) -> p t m j", t=2, j=PACK)
+            if engine == "scalar":
+                nc.scalar.copy(out=dst, in_=src)
+            else:
+                nc.vector.tensor_copy(out=dst, in_=src)
+            staged["w", g, hg, part] = grouped
+
+        def quant_w(g, hg, part):
+            cols = slice(part * 2 * P, (part + 1) * 2 * P)
+            nc.vector.quantize_mx(
+                out=w_codes[g, hg][:, cols].bitcast(E4M3X4),
+                scales=w_plane[g, hg][:, cols],
+                in_=staged["w", g, hg, part][:],
+            )
+
+        def turn_x(pair, banks):
+            for g in range(K_PASSES):
+                staged["xt", pair, g] = bank(banks[g])
+            for a in range(2):
+                words = x_raw[2 * pair + a][:].bitcast(F32).rearrange("r (g p u) -> r g u p", g=K_PASSES, u=2)
+                for g in range(K_PASSES):
+                    for u in range(2):
+                        col = (2 * a + u) * P
+                        nc.tensor.transpose(staged["xt", pair, g][:, col : col + P], words[:, g, u, :], ident[:])
+
+        def drain_x(pair, g):
+            grouped = work.tile([P, PAIR * PACK], BF16, name="x_grouped", tag="x_grouped", bufs=4, align_bytes=64)
+            nc.scalar.copy(
+                out=grouped[:].bitcast(F32).rearrange("p (a r u) -> p a r u", a=2, u=2),
+                in_=staged["xt", pair, g][:].rearrange("p (a u r) -> p a r u", a=2, u=2),
+            )
+            staged["x", pair, g] = grouped
+
+        def quant_x(pair, g):
+            half, part = divmod(pair, 2)
+            cols = slice(part * PAIR, (part + 1) * PAIR)
+            nc.vector.quantize_mx(
+                out=x_codes[g, half][:, cols].bitcast(E4M3X4),
+                scales=x_plane[g, half][:, cols],
+                in_=staged["x", pair, g][:],
+            )
+
+        def z_pass(acc, hg, half, t, g):
+            cols = slice(t * P, (t + 1) * P)
+            nc.tensor.matmul_mx(
+                out=acc[:],
+                lhsT=w_codes[g, hg][:, cols].bitcast(E4M3X4),
+                lhsT_scale=w_plane[g, hg][:, cols],
+                rhs=x_codes[g, half][:].bitcast(E4M3X4),
+                rhs_scale=x_plane[g, half][:],
+                start=(g == 0),
+                stop=(g == K_PASSES - 1),
+            )
+
+        def dz_pass(acc, hg, half, t, g):
+            cols = slice(t * P, (t + 1) * P)
+            nc.tensor.matmul_mx(
+                out=acc[:],
+                lhsT=w_codes[g, hg][:, cols].bitcast(E4M3X4),
+                lhsT_scale=w_plane[g, hg][:, cols],
+                rhs=v_codes[g, half][:].bitcast(E5M2X4),
+                rhs_scale=v_plane[:, g, half * HALF : (half + 1) * HALF],
+                start=(g == 0),
+                stop=(g == K_PASSES - 1),
+            )
+
+        def z_group(acc, hg, half, t):
+            for g in range(K_PASSES):
+                z_pass(acc, hg, half, t, g)
+
+        def dz_group(acc, hg, half, t):
+            for g in range(K_PASSES):
+                dz_pass(acc, hg, half, t, g)
+
+        def slope(z, hg, t):
+            s = work.tile([P, HALF], F32, name="slope", tag="slope", bufs=4)
+            nc.scalar.activation(out=s[:], in_=z[:], func=SIGMOID, bias=bias[:, hg, t : t + 1])
+            return s
+
+        def new_y():
+            return work.tile([P, PACK, HALF], F32, name="y", tag="y", bufs=3)
+
+        def tangent(y, dz, s, hg, t):
+            nc.vector.scalar_tensor_tensor(
+                out=y[:, t, :], in0=dz[:], scalar=dbias[:, hg, t : t + 1], in1=s[:], op0=ADD, op1=MULT
+            )
+
+        def round_y(y):
+            y_bf = work.tile([P, HALF * PACK], BF16, name="y_bf", tag="y_bf", bufs=2, align_bytes=64)
+            nc.vector.tensor_copy(
+                out=y_bf[:].rearrange("p (m t) -> p m t", t=PACK), in_=y[:].rearrange("p t m -> p m t")
+            )
+            return y_bf
+
+        def quant_y(y_bf, hg, half):
+            codes = work.tile([P, HALF], U32, name="y_codes", tag="y_codes", bufs=3, align_bytes=64)
+            nc.vector.quantize_mx(
+                out=codes[:].bitcast(E4M3X4),
+                scales=y_plane[hg][:, half * HALF : (half + 1) * HALF],
+                in_=y_bf[:],
+            )
+            words = out_1[hg].rearrange("p m t -> p (m t)")[:, half * HALF * PACK : (half + 1) * HALF * PACK]
+            nc.sync.dma_start(out=words.bitcast(I32), in_=codes[:].bitcast(I32))
+
+        def store_y_scales(hg):
+            for q in range(4):
+                nc.sync.dma_start(
+                    out=out_2[hg, 4 * q : 4 * q + 4, :].bitcast(I32),
+                    in_=y_plane[hg][32 * q : 32 * q + 4, :].bitcast(I32),
+                )
+
+        def turn_y(y, banks):
+            turned = []
+            for i in range(PACK):
+                yt = bank(banks[i])
+                for t in range(PACK):
+                    nc.tensor.transpose(yt[:, t * P : (t + 1) * P], y[:, t, i * P : (i + 1) * P], ident[:])
+                turned.append(yt)
+            return turned
+
+        def drain_y(yt, hg, half, i):
+            rows = work.tile([P, GROUP], F32, name="y_rows", tag="y_rows", bufs=6)
+            nc.scalar.copy(
+                out=rows[:].rearrange("m (p t) -> m p t", t=PACK), in_=yt[:].rearrange("m (t p) -> m p t", t=PACK)
+            )
+            m0 = half * HALF + i * P
+            nc.sync.dma_start(out=out_0[m0 : m0 + P, hg * GROUP : (hg + 1) * GROUP], in_=rows[:])
+
+        turn_x(0, (4, 5, 6))
+        for g in range(K_PASSES):
+            drain_x(0, g)
+        sort_w(0, 0, 0, "vector")
+        sort_w(0, 0, 1, "vector")
+        quant_w(0, 0, 0)
+        quant_w(0, 0, 1)
+        for g in range(K_PASSES):
+            quant_x(0, g)
+        turn_x(1, (7, 4, 5))
+        for g in range(K_PASSES):
+            drain_x(1, g)
+        quant_x(1, 0)
+        for g in (1, 2):
+            sort_w(g, 0, 0, "vector")
+            sort_w(g, 0, 1, "scalar")
+            quant_x(1, g)
+            quant_w(g, 0, 0)
+            quant_w(g, 0, 1)
+        dz = [bank(t) for t in range(PACK)]
+        z = [bank(b) for b in (6, 7, 4, 5)]
+        for product, acc, g in ((dz_pass, dz, 0), (z_pass, z, 0), (z_pass, z, 1), (dz_pass, dz, 1), (z_pass, z, 2), (dz_pass, dz, 2)):
+            for t in range(PACK):
+                product(acc[t], 0, 0, t, g)
+        y_first = new_y()
+        for t in range(PACK):
+            tangent(y_first, dz[t], slope(z[t], 0, t), 0, t)
+
+        turn_x(2, (6, 7, 4))
+        for g in range(K_PASSES):
+            drain_x(2, g)
+        y_bf = round_y(y_first)
+        quant_x(2, 0)
+        quant_y(y_bf, 0, 0)
+        quant_x(2, 1)
+        quant_x(2, 2)
+        dz = [bank(t) for t in range(PACK)]
+        dz_group(dz[0], 0, 1, 0)
+        dz_group(dz[1], 0, 1, 1)
+        sort_w(0, 1, 0, "vector")
+        sort_w(0, 1, 1, "scalar")
+        turn_x(3, (5, 6, 7))
+        for g in range(K_PASSES):
+            drain_x(3, g)
+        quant_w(0, 1, 0)
+        quant_w(0, 1, 1)
+        sort_w(1, 1, 0, "vector")
+        sort_w(1, 1, 1, "scalar")
+        for g in range(K_PASSES):
+            quant_x(3, g)
+        dz_group(dz[2], 0, 1, 2)
+        dz_group(dz[3], 0, 1, 3)
+        turned = turn_y(y_first, (4, 5, 6, 7))
+        for i in range(PACK):
+            drain_y(turned[i], 0, 0, i)
+        quant_w(1, 1, 0)
+        sort_w(2, 1, 0, "vector")
+        quant_w(1, 1, 1)
+        sort_w(2, 1, 1, "vector")
+        quant_w(2, 1, 0)
+        quant_w(2, 1, 1)
+        y_last = new_y()
+        for t in range(PACK):
+            z = bank(4 + t)
+            z_group(z, 0, 1, t)
+            tangent(y_last, dz[t], slope(z, 0, t), 0, t)
+        last = (0, 1)
+
+        units = [(1, 1), (1, 0), (2, 0), (2, 1)]
+        w_parts = [(g, 2, part) for g in range(K_PASSES) for part in range(2)]
+        for n, (hg, half) in enumerate(units):
+            y = new_y()
+            for t in range(PACK):
+                z = bank(2 * (t % 2))
+                dz1 = bank(2 * (t % 2) + 1)
+                z_group(z, hg, half, t)
+                dz_group(dz1, hg, half, t)
+                s = slope(z, hg, t)
+                if t == 0:
+                    turned = turn_y(y_last, (4, 5, 6, 7))
+                    y_bf = round_y(y_last)
+                tangent(y, dz1, s, hg, t)
+                if t == 0:
+                    quant_y(y_bf, last[0], last[1])
+                    if n % 2 == 0:
+                        store_y_scales(last[0])
+                if t < 2:
+                    drain_y(turned[2 * t], last[0], last[1], 2 * t)
+                    drain_y(turned[2 * t + 1], last[0], last[1], 2 * t + 1)
+                if n < 2:
+                    if t > 0:
+                        quant_w(*w_parts[3 * n + t - 1])
+                    if t < 3:
+                        sort_w(*w_parts[3 * n + t], "vector")
+            y_last, last = y, (hg, half)
+
+        turned = turn_y(y_last, (4, 5, 6, 7))
+        y_bf = round_y(y_last)
+        drain_y(turned[0], last[0], last[1], 0)
+        drain_y(turned[1], last[0], last[1], 1)
+        drain_y(turned[2], last[0], last[1], 2)
+        quant_y(y_bf, last[0], last[1])
+        store_y_scales(last[0])
+        drain_y(turned[3], last[0], last[1], 3)

@@ -25,6 +25,8 @@ H_GROUPS = H // GROUP
 HALF = 512
 HALVES = M // HALF
 PAIR = 256
+LINES = GROUP // 8
+SHARE = 40
 
 
 def tile_softplus_tangent_handoff_k2_kernel(tc, v_words, v_scales, x, w1, b1, db1, out_0, out_1, out_2):
@@ -40,8 +42,15 @@ def tile_softplus_tangent_handoff_k2_kernel(tc, v_words, v_scales, x, w1, b1, db
 
         ident = keep.tile([P, P], F32, name="ident")
         v_plane = keep.tile([P, K_PASSES, M], U8, name="v_plane", align_bytes=64)
-        bias = keep.tile([P, H_GROUPS, PACK], BF16, name="bias")
-        dbias = keep.tile([P, H_GROUPS, PACK], BF16, name="dbias")
+        bias_rows = keep.tile([P, GROUP], BF16, name="bias_rows")
+        bias_words = keep.tile([P, 2, 2 * H_GROUPS], F32, name="bias_words")
+        bias_cols = bias_words[:].rearrange("p u r -> p (u r)").bitcast(BF16)
+
+        def bias_col(row, t):
+            u, e = divmod(t, 2)
+            col = 2 * (u * 2 * H_GROUPS + row) + e
+            return bias_cols[:, col : col + 1]
+
         w_raw, w_codes, w_plane, v_codes, x_raw, x_codes, x_plane, y_plane = {}, {}, {}, {}, {}, {}, {}, {}
         for g in range(K_PASSES):
             for hg in range(H_GROUPS):
@@ -71,24 +80,25 @@ def tile_softplus_tangent_handoff_k2_kernel(tc, v_words, v_scales, x, w1, b1, db
 
         def load_v_scales():
             for q in range(4):
-                nc.sync.dma_start(
+                nc.gpsimd.dma_start(
                     out=v_plane[32 * q : 32 * q + 4, :, :].bitcast(I32),
                     in_=v_scales[:, 4 * q : 4 * q + 4, :].rearrange("g r n -> r g n").bitcast(I32),
                 )
 
         nc.vector.memset(v_plane[:].rearrange("p g n -> p (g n)").bitcast(I32), 0)
+        nc.gpsimd.memset(bias_rows[:], 0.0)
         make_identity(nc, ident[:])
         load_x(0)
         load_w(0, 0)
         load_x(1)
         load_v(0, 0)
+        nc.scalar.dma_start(out=bias_rows[0:H_GROUPS, :], in_=b1.rearrange("(g c) -> g c", c=GROUP))
+        nc.scalar.dma_start(out=bias_rows[H_GROUPS : 2 * H_GROUPS, :], in_=db1.rearrange("(g c) -> g c", c=GROUP))
         load_v_scales()
         load_w(1, 0)
         load_w(2, 0)
         load_v(1, 0)
         load_v(2, 0)
-        nc.sync.dma_start(out=bias[:], in_=b1.rearrange("(g p t) -> p g t", p=P, t=PACK))
-        nc.sync.dma_start(out=dbias[:], in_=db1.rearrange("(g p t) -> p g t", p=P, t=PACK))
         load_x(2)
         for g in range(K_PASSES):
             load_v(g, 1)
@@ -99,22 +109,30 @@ def tile_softplus_tangent_handoff_k2_kernel(tc, v_words, v_scales, x, w1, b1, db
 
         staged = {}
 
-        def sort_w(g, hg, part, engine):
-            grouped = work.tile([P, 2 * GROUP], BF16, name="w_grouped", tag="w_grouped", bufs=4, align_bytes=64)
-            src = w_raw[g, hg][:].rearrange("p j (m t) -> p t m j", t=PACK)[:, 2 * part : 2 * part + 2]
-            dst = grouped[:].rearrange("p (t m j) -> p t m j", t=2, j=PACK)
-            if engine == "scalar":
-                nc.scalar.copy(out=dst, in_=src)
-            else:
-                nc.vector.tensor_copy(out=dst, in_=src)
-            staged["w", g, hg, part] = grouped
+        def sort_w(g, hg, vector_lines):
+            grouped = work.tile([P, PACK * GROUP], BF16, name="w_grouped", tag="w_grouped", bufs=3, align_bytes=64)
+            src = w_raw[g, hg][:].rearrange("p j (c m t) -> p c t m j", m=2, t=PACK)
+            dst = grouped[:].rearrange("p (t c m j) -> p c t m j", t=PACK, m=2, j=PACK)
+            nc.vector.tensor_copy(out=dst[:, :vector_lines], in_=src[:, :vector_lines])
+            if vector_lines < LINES:
+                nc.scalar.copy(out=dst[:, vector_lines:], in_=src[:, vector_lines:])
+            staged["w", g, hg] = grouped
+
+        def turn_bias():
+            words = bias_rows[:].bitcast(F32).rearrange("r (p u) -> r u p", u=2)
+            turned_bias = bank(3)
+            for u in range(2):
+                nc.tensor.transpose(turned_bias[:, u * P : (u + 1) * P], words[:, u, :], ident[:])
+            nc.scalar.copy(
+                out=bias_words[:], in_=turned_bias[:, : 2 * P].rearrange("p (u r) -> p u r", u=2)[:, :, : 2 * H_GROUPS]
+            )
 
         def quant_w(g, hg, part):
             cols = slice(part * 2 * P, (part + 1) * 2 * P)
             nc.vector.quantize_mx(
                 out=w_codes[g, hg][:, cols].bitcast(E4M3X4),
                 scales=w_plane[g, hg][:, cols],
-                in_=staged["w", g, hg, part][:],
+                in_=staged["w", g, hg][:, part * 2 * GROUP : (part + 1) * 2 * GROUP],
             )
 
         def turn_x(pair, banks):
@@ -178,7 +196,7 @@ def tile_softplus_tangent_handoff_k2_kernel(tc, v_words, v_scales, x, w1, b1, db
 
         def slope(z, hg, t):
             s = work.tile([P, HALF], F32, name="slope", tag="slope", bufs=4)
-            nc.scalar.activation(out=s[:], in_=z[:], func=SIGMOID, bias=bias[:, hg, t : t + 1])
+            nc.scalar.activation(out=s[:], in_=z[:], func=SIGMOID, bias=bias_col(hg, t))
             return s
 
         def new_y():
@@ -186,13 +204,14 @@ def tile_softplus_tangent_handoff_k2_kernel(tc, v_words, v_scales, x, w1, b1, db
 
         def tangent(y, dz, s, hg, t):
             nc.vector.scalar_tensor_tensor(
-                out=y[:, t, :], in0=dz[:], scalar=dbias[:, hg, t : t + 1], in1=s[:], op0=ADD, op1=MULT
+                out=y[:, t, :], in0=dz[:], scalar=bias_col(H_GROUPS + hg, t), in1=s[:], op0=ADD, op1=MULT
             )
 
         def round_y(y):
             y_bf = work.tile([P, HALF * PACK], BF16, name="y_bf", tag="y_bf", bufs=2, align_bytes=64)
             nc.vector.tensor_copy(
-                out=y_bf[:].rearrange("p (m t) -> p m t", t=PACK), in_=y[:].rearrange("p t m -> p m t")
+                out=y_bf[:].rearrange("p (c i t) -> p c t i", i=4, t=PACK),
+                in_=y[:].rearrange("p t (c i) -> p c t i", i=4),
             )
             return y_bf
 
@@ -233,19 +252,19 @@ def tile_softplus_tangent_handoff_k2_kernel(tc, v_words, v_scales, x, w1, b1, db
         turn_x(0, (4, 5, 6))
         for g in range(K_PASSES):
             drain_x(0, g)
-        sort_w(0, 0, 0, "vector")
-        sort_w(0, 0, 1, "vector")
+        turn_bias()
+        sort_w(0, 0, LINES)
+        quant_x(0, 0)
         quant_w(0, 0, 0)
         quant_w(0, 0, 1)
-        for g in range(K_PASSES):
-            quant_x(0, g)
+        quant_x(0, 1)
+        quant_x(0, 2)
         turn_x(1, (7, 4, 5))
         for g in range(K_PASSES):
             drain_x(1, g)
         quant_x(1, 0)
         for g in (1, 2):
-            sort_w(g, 0, 0, "vector")
-            sort_w(g, 0, 1, "scalar")
+            sort_w(g, 0, SHARE)
             quant_x(1, g)
             quant_w(g, 0, 0)
             quant_w(g, 0, 1)
@@ -269,15 +288,13 @@ def tile_softplus_tangent_handoff_k2_kernel(tc, v_words, v_scales, x, w1, b1, db
         dz = [bank(t) for t in range(PACK)]
         dz_group(dz[0], 0, 1, 0)
         dz_group(dz[1], 0, 1, 1)
-        sort_w(0, 1, 0, "vector")
-        sort_w(0, 1, 1, "scalar")
+        sort_w(0, 1, SHARE)
         turn_x(3, (5, 6, 7))
         for g in range(K_PASSES):
             drain_x(3, g)
         quant_w(0, 1, 0)
         quant_w(0, 1, 1)
-        sort_w(1, 1, 0, "vector")
-        sort_w(1, 1, 1, "scalar")
+        sort_w(1, 1, SHARE)
         for g in range(K_PASSES):
             quant_x(3, g)
         dz_group(dz[2], 0, 1, 2)
@@ -286,9 +303,8 @@ def tile_softplus_tangent_handoff_k2_kernel(tc, v_words, v_scales, x, w1, b1, db
         for i in range(PACK):
             drain_y(turned[i], 0, 0, i)
         quant_w(1, 1, 0)
-        sort_w(2, 1, 0, "vector")
+        sort_w(2, 1, LINES)
         quant_w(1, 1, 1)
-        sort_w(2, 1, 1, "vector")
         quant_w(2, 1, 0)
         quant_w(2, 1, 1)
         y_last = new_y()
@@ -299,7 +315,8 @@ def tile_softplus_tangent_handoff_k2_kernel(tc, v_words, v_scales, x, w1, b1, db
         last = (0, 1)
 
         units = [(1, 1), (1, 0), (2, 0), (2, 1)]
-        w_parts = [(g, 2, part) for g in range(K_PASSES) for part in range(2)]
+        to_sort = list(range(K_PASSES))
+        to_quantise = []
         for n, (hg, half) in enumerate(units):
             y = new_y()
             for t in range(PACK):
@@ -319,11 +336,14 @@ def tile_softplus_tangent_handoff_k2_kernel(tc, v_words, v_scales, x, w1, b1, db
                 if t < 2:
                     drain_y(turned[2 * t], last[0], last[1], 2 * t)
                     drain_y(turned[2 * t + 1], last[0], last[1], 2 * t + 1)
-                if n < 2:
-                    if t > 0:
-                        quant_w(*w_parts[3 * n + t - 1])
-                    if t < 3:
-                        sort_w(*w_parts[3 * n + t], "vector")
+                if to_quantise:
+                    g = to_quantise.pop()
+                    quant_w(g, 2, 0)
+                    quant_w(g, 2, 1)
+                if t >= 2 and to_sort:
+                    g = to_sort.pop(0)
+                    sort_w(g, 2, SHARE)
+                    to_quantise.append(g)
             y_last, last = y, (hg, half)
 
         turned = turn_y(y_last, (4, 5, 6, 7))

@@ -41,30 +41,29 @@ def tile_softplus_tangent_handoff_k2_kernel(tc, v_words, v_scales, x, w1, b1, db
             return psum.tile([P, HALF], F32, name="bank%d" % i, tag="bank%d" % i)
 
         ident = keep.tile([P, P], F32, name="ident")
-        v_plane = keep.tile([P, K_PASSES, M], U8, name="v_plane", align_bytes=64)
-        bias_rows = keep.tile([P, GROUP], BF16, name="bias_rows")
-        bias_words = keep.tile([P, 2, 2 * H_GROUPS], F32, name="bias_words")
-        bias_cols = bias_words[:].rearrange("p u r -> p (u r)").bitcast(BF16)
+        v_plane = keep.tile([P, K_PASSES, M], U8, name="v_plane", align_bytes=256)
+        bias_first = [keep.tile([P, 1, PACK], BF16, name="bias_first%d" % i) for i in range(2)]
+        bias_rest = [keep.tile([P, H_GROUPS - 1, PACK], BF16, name="bias_rest%d" % i) for i in range(2)]
 
-        def bias_col(row, t):
-            u, e = divmod(t, 2)
-            col = 2 * (u * 2 * H_GROUPS + row) + e
-            return bias_cols[:, col : col + 1]
+        def bias_col(which, hg, t):
+            if hg == 0:
+                return bias_first[which][:, 0, t : t + 1]
+            return bias_rest[which][:, hg - 1, t : t + 1]
 
         w_raw, w_codes, w_plane, v_codes, x_raw, x_codes, x_plane, y_plane = {}, {}, {}, {}, {}, {}, {}, {}
         for g in range(K_PASSES):
             for hg in range(H_GROUPS):
                 w_raw[g, hg] = keep.tile([P, PACK, GROUP], BF16, name="w_raw%d%d" % (g, hg))
-                w_codes[g, hg] = keep.tile([P, GROUP], U32, name="w_codes%d%d" % (g, hg), align_bytes=64)
-                w_plane[g, hg] = keep.tile([P, GROUP], U8, name="w_plane%d%d" % (g, hg), align_bytes=64)
+                w_codes[g, hg] = keep.tile([P, GROUP], U32, name="w_codes%d%d" % (g, hg), align_bytes=256)
+                w_plane[g, hg] = keep.tile([P, GROUP], U8, name="w_plane%d%d" % (g, hg), align_bytes=256)
             for half in range(HALVES):
-                v_codes[g, half] = keep.tile([P, HALF], U32, name="v_codes%d%d" % (g, half), align_bytes=64)
-                x_codes[g, half] = keep.tile([P, HALF], U32, name="x_codes%d%d" % (g, half), align_bytes=64)
-                x_plane[g, half] = keep.tile([P, HALF], U8, name="x_plane%d%d" % (g, half), align_bytes=64)
+                v_codes[g, half] = keep.tile([P, HALF], U32, name="v_codes%d%d" % (g, half), align_bytes=256)
+                x_codes[g, half] = keep.tile([P, HALF], U32, name="x_codes%d%d" % (g, half), align_bytes=256)
+                x_plane[g, half] = keep.tile([P, HALF], U8, name="x_plane%d%d" % (g, half), align_bytes=256)
         for i in range(M // P):
             x_raw[i] = keep.tile([P, D], BF16, name="x_raw%d" % i)
         for hg in range(H_GROUPS):
-            y_plane[hg] = keep.tile([P, M], U8, name="y_plane%d" % hg, align_bytes=64)
+            y_plane[hg] = keep.tile([P, M], U8, name="y_plane%d" % hg, align_bytes=256)
 
         def load_w(g, hg):
             rows = w1[g * GROUP : (g + 1) * GROUP, hg * GROUP : (hg + 1) * GROUP]
@@ -80,25 +79,43 @@ def tile_softplus_tangent_handoff_k2_kernel(tc, v_words, v_scales, x, w1, b1, db
 
         def load_v_scales():
             for q in range(4):
-                nc.gpsimd.dma_start(
+                nc.sync.dma_start(
                     out=v_plane[32 * q : 32 * q + 4, :, :].bitcast(I32),
                     in_=v_scales[:, 4 * q : 4 * q + 4, :].rearrange("g r n -> r g n").bitcast(I32),
                 )
 
+        warm_in = keep.tile([P, PACK * P], BF16, name="warm_in", align_bytes=256)
+        warm_codes = keep.tile([P, P], U32, name="warm_codes", align_bytes=256)
+        warm_plane = keep.tile([P, P], U8, name="warm_plane", align_bytes=256)
+        nc.vector.memset(warm_in[:], 0.0)
         nc.vector.memset(v_plane[:].rearrange("p g n -> p (g n)").bitcast(I32), 0)
-        nc.gpsimd.memset(bias_rows[:], 0.0)
+        nc.vector.quantize_mx(out=warm_codes[:].bitcast(E4M3X4), scales=warm_plane[:], in_=warm_in[:])
+
+        def warm_up(passes):
+            idle = bank(0)
+            for i in range(passes):
+                nc.tensor.matmul_mx(
+                    out=idle[:, :P],
+                    lhsT=warm_codes[:].bitcast(E4M3X4),
+                    lhsT_scale=warm_plane[:],
+                    rhs=warm_codes[:].bitcast(E4M3X4),
+                    rhs_scale=warm_plane[:],
+                    start=True,
+                    stop=True,
+                )
+
         make_identity(nc, ident[:])
         load_x(0)
         load_w(0, 0)
         load_x(1)
         load_v(0, 0)
-        nc.scalar.dma_start(out=bias_rows[0:H_GROUPS, :], in_=b1.rearrange("(g c) -> g c", c=GROUP))
-        nc.scalar.dma_start(out=bias_rows[H_GROUPS : 2 * H_GROUPS, :], in_=db1.rearrange("(g c) -> g c", c=GROUP))
         load_v_scales()
         load_w(1, 0)
         load_w(2, 0)
         load_v(1, 0)
         load_v(2, 0)
+        for which, vec in enumerate((b1, db1)):
+            nc.sync.dma_start(out=bias_first[which][:], in_=vec.rearrange("(g p t) -> p g t", p=P, t=PACK)[:, :1])
         load_x(2)
         for g in range(K_PASSES):
             load_v(g, 1)
@@ -106,26 +123,20 @@ def tile_softplus_tangent_handoff_k2_kernel(tc, v_words, v_scales, x, w1, b1, db
         for hg in range(1, H_GROUPS):
             for g in range(K_PASSES):
                 load_w(g, hg)
+            if hg == 1:
+                for which, vec in enumerate((b1, db1)):
+                    nc.sync.dma_start(out=bias_rest[which][:], in_=vec.rearrange("(g p t) -> p g t", p=P, t=PACK)[:, 1:])
 
         staged = {}
 
         def sort_w(g, hg, vector_lines):
-            grouped = work.tile([P, PACK * GROUP], BF16, name="w_grouped", tag="w_grouped", bufs=3, align_bytes=64)
+            grouped = work.tile([P, PACK * GROUP], BF16, name="w_grouped", tag="w_grouped", bufs=3, align_bytes=256)
             src = w_raw[g, hg][:].rearrange("p j (c m t) -> p c t m j", m=2, t=PACK)
             dst = grouped[:].rearrange("p (t c m j) -> p c t m j", t=PACK, m=2, j=PACK)
             nc.vector.tensor_copy(out=dst[:, :vector_lines], in_=src[:, :vector_lines])
             if vector_lines < LINES:
                 nc.scalar.copy(out=dst[:, vector_lines:], in_=src[:, vector_lines:])
             staged["w", g, hg] = grouped
-
-        def turn_bias():
-            words = bias_rows[:].bitcast(F32).rearrange("r (p u) -> r u p", u=2)
-            turned_bias = bank(3)
-            for u in range(2):
-                nc.tensor.transpose(turned_bias[:, u * P : (u + 1) * P], words[:, u, :], ident[:])
-            nc.scalar.copy(
-                out=bias_words[:], in_=turned_bias[:, : 2 * P].rearrange("p (u r) -> p u r", u=2)[:, :, : 2 * H_GROUPS]
-            )
 
         def quant_w(g, hg, part):
             cols = slice(part * 2 * P, (part + 1) * 2 * P)
@@ -135,18 +146,29 @@ def tile_softplus_tangent_handoff_k2_kernel(tc, v_words, v_scales, x, w1, b1, db
                 in_=staged["w", g, hg][:, part * 2 * GROUP : (part + 1) * 2 * GROUP],
             )
 
-        def turn_x(pair, banks):
+        def x_words(i):
+            return x_raw[i][:].bitcast(F32).rearrange("r (g p u) -> r g u p", g=K_PASSES, u=2)
+
+        def sort_x(pair):
+            for i in (2 * pair, 2 * pair + 1):
+                ordered = work.tile([P, D // 2], F32, name="x_sorted", tag="x_sorted", bufs=4)
+                nc.vector.tensor_copy(
+                    out=ordered[:].rearrange("r (g u c i) -> r g c u i", g=K_PASSES, u=2, i=4),
+                    in_=x_raw[i][:].bitcast(F32).rearrange("r (g c i u) -> r g c u i", g=K_PASSES, u=2, i=4),
+                )
+                staged["xs", i] = ordered[:].rearrange("r (g u p) -> r g u p", g=K_PASSES, u=2)
+
+        def turn_x(pair, banks, words):
             for g in range(K_PASSES):
                 staged["xt", pair, g] = bank(banks[g])
             for a in range(2):
-                words = x_raw[2 * pair + a][:].bitcast(F32).rearrange("r (g p u) -> r g u p", g=K_PASSES, u=2)
                 for g in range(K_PASSES):
                     for u in range(2):
                         col = (2 * a + u) * P
-                        nc.tensor.transpose(staged["xt", pair, g][:, col : col + P], words[:, g, u, :], ident[:])
+                        nc.tensor.transpose(staged["xt", pair, g][:, col : col + P], words[a][:, g, u, :], ident[:])
 
         def drain_x(pair, g):
-            grouped = work.tile([P, PAIR * PACK], BF16, name="x_grouped", tag="x_grouped", bufs=4, align_bytes=64)
+            grouped = work.tile([P, PAIR * PACK], BF16, name="x_grouped", tag="x_grouped", bufs=4, align_bytes=256)
             nc.scalar.copy(
                 out=grouped[:].bitcast(F32).rearrange("p (a r u) -> p a r u", a=2, u=2),
                 in_=staged["xt", pair, g][:].rearrange("p (a u r) -> p a r u", a=2, u=2),
@@ -196,7 +218,7 @@ def tile_softplus_tangent_handoff_k2_kernel(tc, v_words, v_scales, x, w1, b1, db
 
         def slope(z, hg, t):
             s = work.tile([P, HALF], F32, name="slope", tag="slope", bufs=4)
-            nc.scalar.activation(out=s[:], in_=z[:], func=SIGMOID, bias=bias_col(hg, t))
+            nc.scalar.activation(out=s[:], in_=z[:], func=SIGMOID, bias=bias_col(0, hg, t))
             return s
 
         def new_y():
@@ -204,11 +226,11 @@ def tile_softplus_tangent_handoff_k2_kernel(tc, v_words, v_scales, x, w1, b1, db
 
         def tangent(y, dz, s, hg, t):
             nc.vector.scalar_tensor_tensor(
-                out=y[:, t, :], in0=dz[:], scalar=bias_col(H_GROUPS + hg, t), in1=s[:], op0=ADD, op1=MULT
+                out=y[:, t, :], in0=dz[:], scalar=bias_col(1, hg, t), in1=s[:], op0=ADD, op1=MULT
             )
 
         def round_y(y):
-            y_bf = work.tile([P, HALF * PACK], BF16, name="y_bf", tag="y_bf", bufs=2, align_bytes=64)
+            y_bf = work.tile([P, HALF * PACK], BF16, name="y_bf", tag="y_bf", bufs=2, align_bytes=256)
             nc.vector.tensor_copy(
                 out=y_bf[:].rearrange("p (c i t) -> p c t i", i=4, t=PACK),
                 in_=y[:].rearrange("p t (c i) -> p c t i", i=4),
@@ -216,7 +238,7 @@ def tile_softplus_tangent_handoff_k2_kernel(tc, v_words, v_scales, x, w1, b1, db
             return y_bf
 
         def quant_y(y_bf, hg, half):
-            codes = work.tile([P, HALF], U32, name="y_codes", tag="y_codes", bufs=3, align_bytes=64)
+            codes = work.tile([P, HALF], U32, name="y_codes", tag="y_codes", bufs=3, align_bytes=256)
             nc.vector.quantize_mx(
                 out=codes[:].bitcast(E4M3X4),
                 scales=y_plane[hg][:, half * HALF : (half + 1) * HALF],
@@ -241,25 +263,26 @@ def tile_softplus_tangent_handoff_k2_kernel(tc, v_words, v_scales, x, w1, b1, db
                 turned.append(yt)
             return turned
 
-        def drain_y(yt, hg, half, i):
+        def drain_y(yt, hg, half, i, copy=nc.scalar.copy):
             rows = work.tile([P, GROUP], F32, name="y_rows", tag="y_rows", bufs=6)
-            nc.scalar.copy(
+            copy(
                 out=rows[:].rearrange("m (p t) -> m p t", t=PACK), in_=yt[:].rearrange("m (t p) -> m p t", t=PACK)
             )
             m0 = half * HALF + i * P
             nc.sync.dma_start(out=out_0[m0 : m0 + P, hg * GROUP : (hg + 1) * GROUP], in_=rows[:])
 
-        turn_x(0, (4, 5, 6))
+        warm_up(18)
+        turn_x(0, (4, 5, 6), [x_words(0), x_words(1)])
+        warm_up(14)
         for g in range(K_PASSES):
             drain_x(0, g)
-        turn_bias()
         sort_w(0, 0, LINES)
         quant_x(0, 0)
         quant_w(0, 0, 0)
         quant_w(0, 0, 1)
         quant_x(0, 1)
         quant_x(0, 2)
-        turn_x(1, (7, 4, 5))
+        turn_x(1, (7, 4, 5), [x_words(2), x_words(3)])
         for g in range(K_PASSES):
             drain_x(1, g)
         quant_x(1, 0)
@@ -273,23 +296,22 @@ def tile_softplus_tangent_handoff_k2_kernel(tc, v_words, v_scales, x, w1, b1, db
         for product, acc, g in ((dz_pass, dz, 0), (z_pass, z, 0), (z_pass, z, 1), (dz_pass, dz, 1), (z_pass, z, 2), (dz_pass, dz, 2)):
             for t in range(PACK):
                 product(acc[t], 0, 0, t, g)
+        sort_x(2)
         y_first = new_y()
         for t in range(PACK):
             tangent(y_first, dz[t], slope(z[t], 0, t), 0, t)
 
-        turn_x(2, (6, 7, 4))
+        turn_x(2, (6, 7, 4), [staged["xs", 4], staged["xs", 5]])
         for g in range(K_PASSES):
             drain_x(2, g)
-        y_bf = round_y(y_first)
-        quant_x(2, 0)
-        quant_y(y_bf, 0, 0)
-        quant_x(2, 1)
-        quant_x(2, 2)
+        sort_x(3)
+        for g in range(K_PASSES):
+            quant_x(2, g)
         dz = [bank(t) for t in range(PACK)]
         dz_group(dz[0], 0, 1, 0)
         dz_group(dz[1], 0, 1, 1)
         sort_w(0, 1, SHARE)
-        turn_x(3, (5, 6, 7))
+        turn_x(3, (5, 6, 7), [staged["xs", 6], staged["xs", 7]])
         for g in range(K_PASSES):
             drain_x(3, g)
         quant_w(0, 1, 0)
@@ -313,11 +335,13 @@ def tile_softplus_tangent_handoff_k2_kernel(tc, v_words, v_scales, x, w1, b1, db
             z_group(z, 0, 1, t)
             tangent(y_last, dz[t], slope(z, 0, t), 0, t)
         last = (0, 1)
+        owed = [(y_first, 0, 0), (y_last, 0, 1)]
+        halves_done = [0] * H_GROUPS
 
         units = [(1, 1), (1, 0), (2, 0), (2, 1)]
         to_sort = list(range(K_PASSES))
         to_quantise = []
-        for n, (hg, half) in enumerate(units):
+        for hg, half in units:
             y = new_y()
             for t in range(PACK):
                 z = bank(2 * (t % 2))
@@ -327,12 +351,16 @@ def tile_softplus_tangent_handoff_k2_kernel(tc, v_words, v_scales, x, w1, b1, db
                 s = slope(z, hg, t)
                 if t == 0:
                     turned = turn_y(y_last, (4, 5, 6, 7))
-                    y_bf = round_y(y_last)
+                planes_now = owed and (t == 0 or (t == 2 and not to_quantise))
+                if planes_now:
+                    y_owed, hg_owed, half_owed = owed.pop(0)
+                    y_bf = round_y(y_owed)
                 tangent(y, dz1, s, hg, t)
-                if t == 0:
-                    quant_y(y_bf, last[0], last[1])
-                    if n % 2 == 0:
-                        store_y_scales(last[0])
+                if planes_now:
+                    quant_y(y_bf, hg_owed, half_owed)
+                    halves_done[hg_owed] += 1
+                    if halves_done[hg_owed] == HALVES:
+                        store_y_scales(hg_owed)
                 if t < 2:
                     drain_y(turned[2 * t], last[0], last[1], 2 * t)
                     drain_y(turned[2 * t + 1], last[0], last[1], 2 * t + 1)
@@ -340,17 +368,18 @@ def tile_softplus_tangent_handoff_k2_kernel(tc, v_words, v_scales, x, w1, b1, db
                     g = to_quantise.pop()
                     quant_w(g, 2, 0)
                     quant_w(g, 2, 1)
-                if t >= 2 and to_sort:
+                if t in (1, 2) and to_sort:
                     g = to_sort.pop(0)
                     sort_w(g, 2, SHARE)
                     to_quantise.append(g)
             y_last, last = y, (hg, half)
+            owed.append((y, hg, half))
 
         turned = turn_y(y_last, (4, 5, 6, 7))
         y_bf = round_y(y_last)
         drain_y(turned[0], last[0], last[1], 0)
         drain_y(turned[1], last[0], last[1], 1)
         drain_y(turned[2], last[0], last[1], 2)
+        drain_y(turned[3], last[0], last[1], 3, nc.vector.tensor_copy)
         quant_y(y_bf, last[0], last[1])
         store_y_scales(last[0])
-        drain_y(turned[3], last[0], last[1], 3)

@@ -27,6 +27,9 @@ HALVES = M // HALF
 PAIR = 256
 LINES = GROUP // 8
 SHARE = 40
+LATE_SHARE = 48
+FLIP = (1,)
+FD = (2, 3)
 
 
 def tile_softplus_tangent_handoff_k2_kernel(tc, v_words, v_scales, x, w1, b1, db1, out_0, out_1, out_2):
@@ -53,7 +56,7 @@ def tile_softplus_tangent_handoff_k2_kernel(tc, v_words, v_scales, x, w1, b1, db
         w_raw, w_codes, w_plane, v_codes, x_raw, x_codes, x_plane, y_plane = {}, {}, {}, {}, {}, {}, {}, {}
         for g in range(K_PASSES):
             for hg in range(H_GROUPS):
-                w_raw[g, hg] = keep.tile([P, PACK, GROUP], BF16, name="w_raw%d%d" % (g, hg))
+                w_raw[g, hg] = keep.tile([P, PACK, GROUP], BF16, name="w_raw%d%d" % (g, hg), tag="w_raw%d%d" % (g, hg))
                 w_codes[g, hg] = keep.tile([P, GROUP], U32, name="w_codes%d%d" % (g, hg), align_bytes=256)
                 w_plane[g, hg] = keep.tile([P, GROUP], U8, name="w_plane%d%d" % (g, hg), align_bytes=256)
             for half in range(HALVES):
@@ -88,8 +91,8 @@ def tile_softplus_tangent_handoff_k2_kernel(tc, v_words, v_scales, x, w1, b1, db
         warm_codes = keep.tile([P, P], U32, name="warm_codes", align_bytes=256)
         warm_plane = keep.tile([P, P], U8, name="warm_plane", align_bytes=256)
         nc.vector.memset(warm_in[:], 0.0)
-        nc.vector.memset(v_plane[:].rearrange("p g n -> p (g n)").bitcast(I32), 0)
         nc.vector.quantize_mx(out=warm_codes[:].bitcast(E4M3X4), scales=warm_plane[:], in_=warm_in[:])
+        nc.vector.memset(v_plane[:].rearrange("p g n -> p (g n)").bitcast(I32), 0)
 
         def warm_up(passes):
             idle = bank(0)
@@ -222,7 +225,7 @@ def tile_softplus_tangent_handoff_k2_kernel(tc, v_words, v_scales, x, w1, b1, db
             return s
 
         def new_y():
-            return work.tile([P, PACK, HALF], F32, name="y", tag="y", bufs=3)
+            return work.tile([P, PACK, HALF], F32, name="y", tag="y", bufs=3, align_bytes=64)
 
         def tangent(y, dz, s, hg, t):
             nc.vector.scalar_tensor_tensor(
@@ -264,16 +267,33 @@ def tile_softplus_tangent_handoff_k2_kernel(tc, v_words, v_scales, x, w1, b1, db
             return turned
 
         def drain_y(yt, hg, half, i, copy=nc.scalar.copy):
-            rows = work.tile([P, GROUP], F32, name="y_rows", tag="y_rows", bufs=6)
+            rows = work.tile([P, GROUP], F32, name="y_rows", tag="y_rows", bufs=5)
             copy(
                 out=rows[:].rearrange("m (p t) -> m p t", t=PACK), in_=yt[:].rearrange("m (t p) -> m p t", t=PACK)
             )
             m0 = half * HALF + i * P
             nc.sync.dma_start(out=out_0[m0 : m0 + P, hg * GROUP : (hg + 1) * GROUP], in_=rows[:])
 
-        warm_up(18)
+        def flip_y(y, flipped, t):
+            nc.vector.transpose(out=flipped[:, t, :], in_=y[:, t, :])
+
+        spent = ["w_raw%d%d" % (g, hg) for hg in range(2) for g in range(K_PASSES)]
+
+        def drain_flipped(flipped, hg, half, part):
+            rows = keep.tile([P, HALF // 2, PACK], F32, name="flip_rows", tag=spent.pop(0))
+            cols = slice(part * HALF // 2, (part + 1) * HALF // 2)
+            nc.scalar.copy(out=rows[:], in_=flipped[:, :, cols].rearrange("p t n -> p n t"))
+            m0 = half * HALF + part * HALF // 2
+            for q in range(4):
+                h0 = hg * GROUP + q * P
+                nc.sync.dma_start(
+                    out=out_0[m0 : m0 + HALF // 2, h0 : h0 + P].rearrange("(b i) h -> i b h", i=32),
+                    in_=rows[32 * q : 32 * q + 32].rearrange("i (b j) t -> i b (j t)", j=32),
+                )
+
+        warm_up(12)
         turn_x(0, (4, 5, 6), [x_words(0), x_words(1)])
-        warm_up(14)
+        warm_up(12)
         for g in range(K_PASSES):
             drain_x(0, g)
         sort_w(0, 0, LINES)
@@ -341,17 +361,27 @@ def tile_softplus_tangent_handoff_k2_kernel(tc, v_words, v_scales, x, w1, b1, db
         units = [(1, 1), (1, 0), (2, 0), (2, 1)]
         to_sort = list(range(K_PASSES))
         to_quantise = []
-        for hg, half in units:
+        flipped_last = None
+        for n, (hg, half) in enumerate(units):
             y = new_y()
+            flipped = None
+            if n in FLIP:
+                flipped = work.tile([P, PACK, HALF], F32, name="flipped", tag="flipped", bufs=2, align_bytes=64)
             for t in range(PACK):
-                z = bank(2 * (t % 2))
-                dz1 = bank(2 * (t % 2) + 1)
+                first_bank = 2 * (t % 2) + (4 if flipped_last is not None and t < 2 else 0)
+                z = bank(first_bank)
+                dz1 = bank(first_bank + 1)
                 z_group(z, hg, half, t)
                 dz_group(dz1, hg, half, t)
                 s = slope(z, hg, t)
-                if t == 0:
+                if t == 0 and flipped_last is None:
                     turned = turn_y(y_last, (4, 5, 6, 7))
-                planes_now = owed and (t == 0 or (t == 2 and not to_quantise))
+                if t < 2 and flipped_last is None:
+                    drain_y(turned[2 * t], last[0], last[1], 2 * t)
+                    drain_y(turned[2 * t + 1], last[0], last[1], 2 * t + 1)
+                if t in FD and flipped_last is not None:
+                    drain_flipped(flipped_last, last[0], last[1], FD.index(t))
+                planes_now = t == 0 or (t == 2 and n == len(units) - 1)
                 if planes_now:
                     y_owed, hg_owed, half_owed = owed.pop(0)
                     y_bf = round_y(y_owed)
@@ -361,17 +391,19 @@ def tile_softplus_tangent_handoff_k2_kernel(tc, v_words, v_scales, x, w1, b1, db
                     halves_done[hg_owed] += 1
                     if halves_done[hg_owed] == HALVES:
                         store_y_scales(hg_owed)
-                if t < 2:
-                    drain_y(turned[2 * t], last[0], last[1], 2 * t)
-                    drain_y(turned[2 * t + 1], last[0], last[1], 2 * t + 1)
                 if to_quantise:
                     g = to_quantise.pop()
                     quant_w(g, 2, 0)
                     quant_w(g, 2, 1)
                 if t in (1, 2) and to_sort:
                     g = to_sort.pop(0)
-                    sort_w(g, 2, SHARE)
+                    sort_w(g, 2, LATE_SHARE)
                     to_quantise.append(g)
+                if flipped is not None and t > 0:
+                    flip_y(y, flipped, t - 1)
+                if flipped_last is not None and t == 0:
+                    flip_y(y_last, flipped_last, PACK - 1)
+            flipped_last = flipped
             y_last, last = y, (hg, half)
             owed.append((y, hg, half))
 

@@ -24,12 +24,19 @@ K_PASSES = D // GROUP
 H_GROUPS = H // GROUP
 HALF = 512
 HALVES = M // HALF
-PAIR = 256
-LINES = GROUP // 8
-SHARE = 40
-LATE_SHARE = 48
-FLIP = (1,)
-FD = (2, 3)
+PAIR = 2 * P
+QUADRANT = 32
+QUADRANTS = P // QUADRANT
+SCALE_ROWS = 4
+ALIGN = 256
+
+W_RUNS = GROUP // 8
+W_VECTOR_RUNS = 48
+Y_RUNS = HALF // 4
+WARM_PASSES = 12
+
+LOW_PAIRS = (0, 2)
+HIGH_BANKS = (4, 5, 6, 7)
 
 
 def tile_softplus_tangent_handoff_k2_kernel(tc, v_words, v_scales, x, w1, b1, db1, out_0, out_1, out_2):
@@ -44,7 +51,7 @@ def tile_softplus_tangent_handoff_k2_kernel(tc, v_words, v_scales, x, w1, b1, db
             return psum.tile([P, HALF], F32, name="bank%d" % i, tag="bank%d" % i)
 
         ident = keep.tile([P, P], F32, name="ident")
-        v_plane = keep.tile([P, K_PASSES, M], U8, name="v_plane", align_bytes=256)
+        v_plane = keep.tile([P, K_PASSES, M], U8, name="v_plane", align_bytes=ALIGN)
         bias_first = [keep.tile([P, 1, PACK], BF16, name="bias_first%d" % i) for i in range(2)]
         bias_rest = [keep.tile([P, H_GROUPS - 1, PACK], BF16, name="bias_rest%d" % i) for i in range(2)]
 
@@ -57,16 +64,16 @@ def tile_softplus_tangent_handoff_k2_kernel(tc, v_words, v_scales, x, w1, b1, db
         for g in range(K_PASSES):
             for hg in range(H_GROUPS):
                 w_raw[g, hg] = keep.tile([P, PACK, GROUP], BF16, name="w_raw%d%d" % (g, hg), tag="w_raw%d%d" % (g, hg))
-                w_codes[g, hg] = keep.tile([P, GROUP], U32, name="w_codes%d%d" % (g, hg), align_bytes=256)
-                w_plane[g, hg] = keep.tile([P, GROUP], U8, name="w_plane%d%d" % (g, hg), align_bytes=256)
+                w_codes[g, hg] = keep.tile([P, GROUP], U32, name="w_codes%d%d" % (g, hg), align_bytes=ALIGN)
+                w_plane[g, hg] = keep.tile([P, GROUP], U8, name="w_plane%d%d" % (g, hg), align_bytes=ALIGN)
             for half in range(HALVES):
-                v_codes[g, half] = keep.tile([P, HALF], U32, name="v_codes%d%d" % (g, half), align_bytes=256)
-                x_codes[g, half] = keep.tile([P, HALF], U32, name="x_codes%d%d" % (g, half), align_bytes=256)
-                x_plane[g, half] = keep.tile([P, HALF], U8, name="x_plane%d%d" % (g, half), align_bytes=256)
+                v_codes[g, half] = keep.tile([P, HALF], U32, name="v_codes%d%d" % (g, half), align_bytes=ALIGN)
+                x_codes[g, half] = keep.tile([P, HALF], U32, name="x_codes%d%d" % (g, half), align_bytes=ALIGN)
+                x_plane[g, half] = keep.tile([P, HALF], U8, name="x_plane%d%d" % (g, half), align_bytes=ALIGN)
         for i in range(M // P):
             x_raw[i] = keep.tile([P, D], BF16, name="x_raw%d" % i)
         for hg in range(H_GROUPS):
-            y_plane[hg] = keep.tile([P, M], U8, name="y_plane%d" % hg, align_bytes=256)
+            y_plane[hg] = keep.tile([P, M], U8, name="y_plane%d" % hg, align_bytes=ALIGN)
 
         def load_w(g, hg):
             rows = w1[g * GROUP : (g + 1) * GROUP, hg * GROUP : (hg + 1) * GROUP]
@@ -81,22 +88,26 @@ def tile_softplus_tangent_handoff_k2_kernel(tc, v_words, v_scales, x, w1, b1, db
                 nc.sync.dma_start(out=x_raw[i][:], in_=x[i * P : (i + 1) * P, :])
 
         def load_v_scales():
-            for q in range(4):
+            for q in range(QUADRANTS):
                 nc.sync.dma_start(
-                    out=v_plane[32 * q : 32 * q + 4, :, :].bitcast(I32),
-                    in_=v_scales[:, 4 * q : 4 * q + 4, :].rearrange("g r n -> r g n").bitcast(I32),
+                    out=v_plane[QUADRANT * q : QUADRANT * q + SCALE_ROWS, :, :].bitcast(I32),
+                    in_=v_scales[:, SCALE_ROWS * q : SCALE_ROWS * (q + 1), :].rearrange("g r n -> r g n").bitcast(I32),
                 )
 
-        warm_in = keep.tile([P, PACK * P], BF16, name="warm_in", align_bytes=256)
-        warm_codes = keep.tile([P, P], U32, name="warm_codes", align_bytes=256)
-        warm_plane = keep.tile([P, P], U8, name="warm_plane", align_bytes=256)
+        def load_biases(tiles, groups):
+            for which, vec in enumerate((b1, db1)):
+                nc.sync.dma_start(out=tiles[which][:], in_=vec.rearrange("(g p t) -> p g t", p=P, t=PACK)[:, groups])
+
+        warm_in = keep.tile([P, PACK * P], BF16, name="warm_in", align_bytes=ALIGN)
+        warm_codes = keep.tile([P, P], U32, name="warm_codes", align_bytes=ALIGN)
+        warm_plane = keep.tile([P, P], U8, name="warm_plane", align_bytes=ALIGN)
         nc.vector.memset(warm_in[:], 0.0)
         nc.vector.quantize_mx(out=warm_codes[:].bitcast(E4M3X4), scales=warm_plane[:], in_=warm_in[:])
         nc.vector.memset(v_plane[:].rearrange("p g n -> p (g n)").bitcast(I32), 0)
 
-        def warm_up(passes):
+        def warm_up():
             idle = bank(0)
-            for i in range(passes):
+            for i in range(WARM_PASSES):
                 nc.tensor.matmul_mx(
                     out=idle[:, :P],
                     lhsT=warm_codes[:].bitcast(E4M3X4),
@@ -117,66 +128,70 @@ def tile_softplus_tangent_handoff_k2_kernel(tc, v_words, v_scales, x, w1, b1, db
         load_w(2, 0)
         load_v(1, 0)
         load_v(2, 0)
-        for which, vec in enumerate((b1, db1)):
-            nc.sync.dma_start(out=bias_first[which][:], in_=vec.rearrange("(g p t) -> p g t", p=P, t=PACK)[:, :1])
+        load_biases(bias_first, slice(0, 1))
         load_x(2)
         for g in range(K_PASSES):
             load_v(g, 1)
         load_x(3)
-        for hg in range(1, H_GROUPS):
-            for g in range(K_PASSES):
-                load_w(g, hg)
-            if hg == 1:
-                for which, vec in enumerate((b1, db1)):
-                    nc.sync.dma_start(out=bias_rest[which][:], in_=vec.rearrange("(g p t) -> p g t", p=P, t=PACK)[:, 1:])
+        for g in range(K_PASSES):
+            load_w(g, 1)
+        load_biases(bias_rest, slice(1, H_GROUPS))
+        for g in range(K_PASSES):
+            load_w(g, 2)
 
-        staged = {}
+        w_grouped, x_turned, x_grouped = {}, {}, {}
 
-        def sort_w(g, hg, vector_lines):
-            grouped = work.tile([P, PACK * GROUP], BF16, name="w_grouped", tag="w_grouped", bufs=3, align_bytes=256)
+        def sort_w(g, hg, vector_runs):
+            grouped = work.tile([P, PACK * GROUP], BF16, name="w_grouped", tag="w_grouped", bufs=3, align_bytes=ALIGN)
             src = w_raw[g, hg][:].rearrange("p j (c m t) -> p c t m j", m=2, t=PACK)
             dst = grouped[:].rearrange("p (t c m j) -> p c t m j", t=PACK, m=2, j=PACK)
-            nc.vector.tensor_copy(out=dst[:, :vector_lines], in_=src[:, :vector_lines])
-            if vector_lines < LINES:
-                nc.scalar.copy(out=dst[:, vector_lines:], in_=src[:, vector_lines:])
-            staged["w", g, hg] = grouped
+            nc.vector.tensor_copy(out=dst[:, :vector_runs], in_=src[:, :vector_runs])
+            if vector_runs < W_RUNS:
+                nc.scalar.copy(out=dst[:, vector_runs:], in_=src[:, vector_runs:])
+            w_grouped[g, hg] = grouped
 
-        def quant_w(g, hg, part):
-            cols = slice(part * 2 * P, (part + 1) * 2 * P)
+        def quant_w(g, hg, slots=slice(0, PACK)):
+            cols = slice(slots.start * P, slots.stop * P)
             nc.vector.quantize_mx(
                 out=w_codes[g, hg][:, cols].bitcast(E4M3X4),
                 scales=w_plane[g, hg][:, cols],
-                in_=staged["w", g, hg][:, part * 2 * GROUP : (part + 1) * 2 * GROUP],
+                in_=w_grouped[g, hg][:, slots.start * GROUP : slots.stop * GROUP],
             )
 
-        def x_words(i):
+        def quant_w_by_halves(g):
+            quant_w(g, 0, slice(0, 2))
+            quant_w(g, 0, slice(2, PACK))
+
+        def x_pairs(i):
             return x_raw[i][:].bitcast(F32).rearrange("r (g p u) -> r g u p", g=K_PASSES, u=2)
 
         def sort_x(pair):
+            views = []
             for i in (2 * pair, 2 * pair + 1):
                 ordered = work.tile([P, D // 2], F32, name="x_sorted", tag="x_sorted", bufs=4)
                 nc.vector.tensor_copy(
                     out=ordered[:].rearrange("r (g u c i) -> r g c u i", g=K_PASSES, u=2, i=4),
                     in_=x_raw[i][:].bitcast(F32).rearrange("r (g c i u) -> r g c u i", g=K_PASSES, u=2, i=4),
                 )
-                staged["xs", i] = ordered[:].rearrange("r (g u p) -> r g u p", g=K_PASSES, u=2)
+                views.append(ordered[:].rearrange("r (g u p) -> r g u p", g=K_PASSES, u=2))
+            return views
 
-        def turn_x(pair, banks, words):
+        def turn_x(pair, banks, views):
             for g in range(K_PASSES):
-                staged["xt", pair, g] = bank(banks[g])
+                x_turned[pair, g] = bank(banks[g])
             for a in range(2):
                 for g in range(K_PASSES):
                     for u in range(2):
                         col = (2 * a + u) * P
-                        nc.tensor.transpose(staged["xt", pair, g][:, col : col + P], words[a][:, g, u, :], ident[:])
+                        nc.tensor.transpose(x_turned[pair, g][:, col : col + P], views[a][:, g, u, :], ident[:])
 
         def drain_x(pair, g):
-            grouped = work.tile([P, PAIR * PACK], BF16, name="x_grouped", tag="x_grouped", bufs=4, align_bytes=256)
+            grouped = work.tile([P, PAIR * PACK], BF16, name="x_grouped", tag="x_grouped", bufs=4, align_bytes=ALIGN)
             nc.scalar.copy(
                 out=grouped[:].bitcast(F32).rearrange("p (a r u) -> p a r u", a=2, u=2),
-                in_=staged["xt", pair, g][:].rearrange("p (a u r) -> p a r u", a=2, u=2),
+                in_=x_turned[pair, g][:].rearrange("p (a u r) -> p a r u", a=2, u=2),
             )
-            staged["x", pair, g] = grouped
+            x_grouped[pair, g] = grouped
 
         def quant_x(pair, g):
             half, part = divmod(pair, 2)
@@ -184,7 +199,7 @@ def tile_softplus_tangent_handoff_k2_kernel(tc, v_words, v_scales, x, w1, b1, db
             nc.vector.quantize_mx(
                 out=x_codes[g, half][:, cols].bitcast(E4M3X4),
                 scales=x_plane[g, half][:, cols],
-                in_=staged["x", pair, g][:],
+                in_=x_grouped[pair, g][:],
             )
 
         def z_pass(acc, hg, half, t, g):
@@ -232,16 +247,17 @@ def tile_softplus_tangent_handoff_k2_kernel(tc, v_words, v_scales, x, w1, b1, db
                 out=y[:, t, :], in0=dz[:], scalar=bias_col(1, hg, t), in1=s[:], op0=ADD, op1=MULT
             )
 
-        def round_y(y):
-            y_bf = work.tile([P, HALF * PACK], BF16, name="y_bf", tag="y_bf", bufs=2, align_bytes=256)
-            nc.vector.tensor_copy(
-                out=y_bf[:].rearrange("p (c i t) -> p c t i", i=4, t=PACK),
-                in_=y[:].rearrange("p t (c i) -> p c t i", i=4),
-            )
+        def round_y(y, vector_runs):
+            y_bf = work.tile([P, HALF * PACK], BF16, name="y_bf", tag="y_bf", bufs=2, align_bytes=ALIGN)
+            dst = y_bf[:].rearrange("p (c i t) -> p c t i", i=4, t=PACK)
+            src = y[:].rearrange("p t (c i) -> p c t i", i=4)
+            nc.vector.tensor_copy(out=dst[:, :vector_runs], in_=src[:, :vector_runs])
+            if vector_runs < Y_RUNS:
+                nc.scalar.copy(out=dst[:, vector_runs:], in_=src[:, vector_runs:])
             return y_bf
 
         def quant_y(y_bf, hg, half):
-            codes = work.tile([P, HALF], U32, name="y_codes", tag="y_codes", bufs=3, align_bytes=256)
+            codes = work.tile([P, HALF], U32, name="y_codes", tag="y_codes", bufs=3, align_bytes=ALIGN)
             nc.vector.quantize_mx(
                 out=codes[:].bitcast(E4M3X4),
                 scales=y_plane[hg][:, half * HALF : (half + 1) * HALF],
@@ -251,24 +267,24 @@ def tile_softplus_tangent_handoff_k2_kernel(tc, v_words, v_scales, x, w1, b1, db
             nc.sync.dma_start(out=words.bitcast(I32), in_=codes[:].bitcast(I32))
 
         def store_y_scales(hg):
-            for q in range(4):
+            for q in range(QUADRANTS):
                 nc.sync.dma_start(
-                    out=out_2[hg, 4 * q : 4 * q + 4, :].bitcast(I32),
-                    in_=y_plane[hg][32 * q : 32 * q + 4, :].bitcast(I32),
+                    out=out_2[hg, SCALE_ROWS * q : SCALE_ROWS * (q + 1), :].bitcast(I32),
+                    in_=y_plane[hg][QUADRANT * q : QUADRANT * q + SCALE_ROWS, :].bitcast(I32),
                 )
 
         def turn_y(y, banks):
             turned = []
-            for i in range(PACK):
+            for i in range(HALF // P):
                 yt = bank(banks[i])
                 for t in range(PACK):
                     nc.tensor.transpose(yt[:, t * P : (t + 1) * P], y[:, t, i * P : (i + 1) * P], ident[:])
                 turned.append(yt)
             return turned
 
-        def drain_y(yt, hg, half, i, copy=nc.scalar.copy):
+        def drain_y(yt, hg, half, i):
             rows = work.tile([P, GROUP], F32, name="y_rows", tag="y_rows", bufs=5)
-            copy(
+            nc.scalar.copy(
                 out=rows[:].rearrange("m (p t) -> m p t", t=PACK), in_=yt[:].rearrange("m (t p) -> m p t", t=PACK)
             )
             m0 = half * HALF + i * P
@@ -277,127 +293,135 @@ def tile_softplus_tangent_handoff_k2_kernel(tc, v_words, v_scales, x, w1, b1, db
         def flip_y(y, flipped, t):
             nc.vector.transpose(out=flipped[:, t, :], in_=y[:, t, :])
 
-        spent = ["w_raw%d%d" % (g, hg) for hg in range(2) for g in range(K_PASSES)]
-
         def drain_flipped(flipped, hg, half, part):
-            rows = keep.tile([P, HALF // 2, PACK], F32, name="flip_rows", tag=spent.pop(0))
+            rows = keep.tile([P, HALF // 2, PACK], F32, name="flip_rows", tag="w_raw%d0" % part)
             cols = slice(part * HALF // 2, (part + 1) * HALF // 2)
             nc.scalar.copy(out=rows[:], in_=flipped[:, :, cols].rearrange("p t n -> p n t"))
             m0 = half * HALF + part * HALF // 2
-            for q in range(4):
+            for q in range(QUADRANTS):
                 h0 = hg * GROUP + q * P
                 nc.sync.dma_start(
-                    out=out_0[m0 : m0 + HALF // 2, h0 : h0 + P].rearrange("(b i) h -> i b h", i=32),
-                    in_=rows[32 * q : 32 * q + 32].rearrange("i (b j) t -> i b (j t)", j=32),
+                    out=out_0[m0 : m0 + HALF // 2, h0 : h0 + P].rearrange("(b i) h -> i b h", i=QUADRANT),
+                    in_=rows[QUADRANT * q : QUADRANT * (q + 1)].rearrange("i (b j) t -> i b (j t)", j=QUADRANT),
                 )
 
-        warm_up(12)
-        turn_x(0, (4, 5, 6), [x_words(0), x_words(1)])
-        warm_up(12)
+        warm_up()
+        turn_x(0, (4, 5, 6), [x_pairs(0), x_pairs(1)])
+        warm_up()
         for g in range(K_PASSES):
             drain_x(0, g)
-        sort_w(0, 0, LINES)
+        sort_w(0, 0, W_RUNS)
         quant_x(0, 0)
-        quant_w(0, 0, 0)
-        quant_w(0, 0, 1)
+        quant_w_by_halves(0)
         quant_x(0, 1)
         quant_x(0, 2)
-        turn_x(1, (7, 4, 5), [x_words(2), x_words(3)])
+        turn_x(1, (7, 4, 5), [x_pairs(2), x_pairs(3)])
         for g in range(K_PASSES):
             drain_x(1, g)
         quant_x(1, 0)
         for g in (1, 2):
-            sort_w(g, 0, SHARE)
+            sort_w(g, 0, W_VECTOR_RUNS)
             quant_x(1, g)
-            quant_w(g, 0, 0)
-            quant_w(g, 0, 1)
+            quant_w_by_halves(g)
         dz = [bank(t) for t in range(PACK)]
         z = [bank(b) for b in (6, 7, 4, 5)]
-        for product, acc, g in ((dz_pass, dz, 0), (z_pass, z, 0), (z_pass, z, 1), (dz_pass, dz, 1), (z_pass, z, 2), (dz_pass, dz, 2)):
+        for product, acc, g in (
+            (dz_pass, dz, 0),
+            (z_pass, z, 0),
+            (z_pass, z, 1),
+            (dz_pass, dz, 1),
+            (z_pass, z, 2),
+            (dz_pass, dz, 2),
+        ):
             for t in range(PACK):
                 product(acc[t], 0, 0, t, g)
-        sort_x(2)
+        views = sort_x(2)
         y_first = new_y()
         for t in range(PACK):
             tangent(y_first, dz[t], slope(z[t], 0, t), 0, t)
 
-        turn_x(2, (6, 7, 4), [staged["xs", 4], staged["xs", 5]])
+        turn_x(2, (6, 7, 4), views)
         for g in range(K_PASSES):
             drain_x(2, g)
-        sort_x(3)
+        views = sort_x(3)
         for g in range(K_PASSES):
             quant_x(2, g)
         dz = [bank(t) for t in range(PACK)]
         dz_group(dz[0], 0, 1, 0)
         dz_group(dz[1], 0, 1, 1)
-        sort_w(0, 1, SHARE)
-        turn_x(3, (5, 6, 7), [staged["xs", 6], staged["xs", 7]])
+        sort_w(0, 1, W_VECTOR_RUNS)
+        turn_x(3, (5, 6, 7), views)
         for g in range(K_PASSES):
             drain_x(3, g)
-        quant_w(0, 1, 0)
-        quant_w(0, 1, 1)
-        sort_w(1, 1, SHARE)
-        for g in range(K_PASSES):
             quant_x(3, g)
+            if g == 0:
+                quant_w(0, 1)
+        sort_w(1, 1, W_VECTOR_RUNS)
         dz_group(dz[2], 0, 1, 2)
         dz_group(dz[3], 0, 1, 3)
-        turned = turn_y(y_first, (4, 5, 6, 7))
-        for i in range(PACK):
+        turned = turn_y(y_first, HIGH_BANKS)
+        for i in range(HALF // P):
             drain_y(turned[i], 0, 0, i)
-        quant_w(1, 1, 0)
-        sort_w(2, 1, LINES)
-        quant_w(1, 1, 1)
-        quant_w(2, 1, 0)
-        quant_w(2, 1, 1)
+        sort_w(2, 1, W_VECTOR_RUNS)
+        quant_w(1, 1)
+        quant_w(2, 1)
         y_last = new_y()
         for t in range(PACK):
-            z = bank(4 + t)
-            z_group(z, 0, 1, t)
-            tangent(y_last, dz[t], slope(z, 0, t), 0, t)
-        last = (0, 1)
-        owed = [(y_first, 0, 0), (y_last, 0, 1)]
-        halves_done = [0] * H_GROUPS
+            z_slot = bank(HIGH_BANKS[t])
+            z_group(z_slot, 0, 1, t)
+            tangent(y_last, dz[t], slope(z_slot, 0, t), 0, t)
 
         units = [(1, 1), (1, 0), (2, 0), (2, 1)]
+        flipped_unit = (1, 0)
+        last = (0, 1)
+        flipped_last = None
+        owed = [(y_first, 0, 0), (y_last, 0, 1)]
+        rounded = []
+        halves_done = [0] * H_GROUPS
         to_sort = list(range(K_PASSES))
         to_quantise = []
-        flipped_last = None
         for n, (hg, half) in enumerate(units):
             y = new_y()
             flipped = None
-            if n in FLIP:
-                flipped = work.tile([P, PACK, HALF], F32, name="flipped", tag="flipped", bufs=2, align_bytes=64)
+            if (hg, half) == flipped_unit:
+                flipped = work.tile([P, PACK, HALF], F32, name="flipped", tag="flipped", bufs=1, align_bytes=64)
             for t in range(PACK):
-                first_bank = 2 * (t % 2) + (4 if flipped_last is not None and t < 2 else 0)
-                z = bank(first_bank)
-                dz1 = bank(first_bank + 1)
-                z_group(z, hg, half, t)
-                dz_group(dz1, hg, half, t)
-                s = slope(z, hg, t)
-                if t == 0 and flipped_last is None:
-                    turned = turn_y(y_last, (4, 5, 6, 7))
-                if t < 2 and flipped_last is None:
-                    drain_y(turned[2 * t], last[0], last[1], 2 * t)
-                    drain_y(turned[2 * t + 1], last[0], last[1], 2 * t + 1)
-                if t in FD and flipped_last is not None:
-                    drain_flipped(flipped_last, last[0], last[1], FD.index(t))
-                planes_now = t == 0 or (t == 2 and n == len(units) - 1)
-                if planes_now:
-                    y_owed, hg_owed, half_owed = owed.pop(0)
-                    y_bf = round_y(y_owed)
-                tangent(y, dz1, s, hg, t)
-                if planes_now:
+                first_bank = LOW_PAIRS[(t + n) % 2]
+                if t == 3:
+                    first_bank = HIGH_BANKS[0]
+                if t == 2 and flipped_last is not None:
+                    first_bank = HIGH_BANKS[2]
+                z_slot = bank(first_bank)
+                dz_slot = bank(first_bank + 1)
+                z_group(z_slot, hg, half, t)
+                dz_group(dz_slot, hg, half, t)
+                s = slope(z_slot, hg, t)
+                if flipped_last is None:
+                    if t == 1:
+                        turned = turn_y(y_last, HIGH_BANKS)
+                        drain_y(turned[0], last[0], last[1], 0)
+                    if t >= 1:
+                        drain_y(turned[t], last[0], last[1], t)
+                elif t >= 2:
+                    drain_flipped(flipped_last, last[0], last[1], t - 2)
+                tangent(y, dz_slot, s, hg, t)
+                if rounded:
+                    y_bf, hg_owed, half_owed = rounded.pop()
                     quant_y(y_bf, hg_owed, half_owed)
                     halves_done[hg_owed] += 1
                     if halves_done[hg_owed] == HALVES:
                         store_y_scales(hg_owed)
+                if t == 0:
+                    y_owed, hg_owed, half_owed = owed.pop(0)
+                    rounded.append((round_y(y_owed, Y_RUNS // 2), hg_owed, half_owed))
+                if t == 2 and flipped_last is not None:
+                    y_owed, hg_owed, half_owed = owed.pop(0)
+                    rounded.append((round_y(y_owed, Y_RUNS), hg_owed, half_owed))
                 if to_quantise:
-                    g = to_quantise.pop()
-                    quant_w(g, 2, 0)
-                    quant_w(g, 2, 1)
+                    quant_w(to_quantise.pop(), 2)
                 if t in (1, 2) and to_sort:
                     g = to_sort.pop(0)
-                    sort_w(g, 2, LATE_SHARE)
+                    sort_w(g, 2, W_VECTOR_RUNS)
                     to_quantise.append(g)
                 if flipped is not None and t > 0:
                     flip_y(y, flipped, t - 1)
@@ -407,11 +431,10 @@ def tile_softplus_tangent_handoff_k2_kernel(tc, v_words, v_scales, x, w1, b1, db
             y_last, last = y, (hg, half)
             owed.append((y, hg, half))
 
-        turned = turn_y(y_last, (4, 5, 6, 7))
-        y_bf = round_y(y_last)
-        drain_y(turned[0], last[0], last[1], 0)
-        drain_y(turned[1], last[0], last[1], 1)
-        drain_y(turned[2], last[0], last[1], 2)
-        drain_y(turned[3], last[0], last[1], 3, nc.vector.tensor_copy)
+        turned = turn_y(y_last, (0, 1, 6, 7))
+        y_bf = round_y(y_last, Y_RUNS)
+        for i in range(HALF // P - 1):
+            drain_y(turned[i], last[0], last[1], i)
         quant_y(y_bf, last[0], last[1])
+        drain_y(turned[-1], last[0], last[1], HALF // P - 1)
         store_y_scales(last[0])

from contextlib import ExitStack

import concourse.mybir as mybir
from concourse.masks import make_identity

M, D, H = 1024, 1536, 1536
FLOPS = 2 * 2 * M * D * H

F32 = mybir.dt.float32
BF16 = mybir.dt.bfloat16
I32 = mybir.dt.int32
U32 = mybir.dt.uint32
U8 = mybir.dt.uint8
E4M3X4 = mybir.dt.float8_e4m3fn_x4
E5M2X4 = mybir.dt.float8_e5m2_x4
SIGMOID = mybir.ActivationFunctionType.Sigmoid
ADD = mybir.AluOpType.add
MULT = mybir.AluOpType.mult

P = 128
PACK = 4
GROUP = P * PACK
K_PASSES = D // GROUP
H_GROUPS = H // GROUP
HALF = 512
HALVES = M // HALF
PAIR = 2 * P
QUADRANT = 32
QUADRANTS = P // QUADRANT
SCALE_ROWS = 4
ALIGN = 256

W_RUNS = GROUP // 8
W_VECTOR_RUNS = 48
Y_RUNS = HALF // 4
WARM_PASSES = 12

LOW_PAIRS = (0, 2)
HIGH_BANKS = (4, 5, 6, 7)


def tile_softplus_tangent_handoff_k2_kernel(tc, v_words, v_scales, x, w1, b1, db1, out_0, out_1, out_2):
    nc = tc.nc
    with ExitStack() as ctx:
        keep = ctx.enter_context(tc.tile_pool(name="keep", bufs=1))
        work = ctx.enter_context(tc.tile_pool(name="work", bufs=3))
        psum = ctx.enter_context(tc.psum_pool(name="psum", bufs=1))
        ctx.enter_context(tc.manual_schedule())

        def bank(i):
            return psum.tile([P, HALF], F32, name="bank%d" % i, tag="bank%d" % i)

        ident = keep.tile([P, P], F32, name="ident")
        v_plane = keep.tile([P, K_PASSES, M], U8, name="v_plane", align_bytes=ALIGN)
        bias_first = [keep.tile([P, 1, PACK], BF16, name="bias_first%d" % i) for i in range(2)]
        bias_rest = [keep.tile([P, H_GROUPS - 1, PACK], BF16, name="bias_rest%d" % i) for i in range(2)]

        def bias_col(which, hg, t):
            if hg == 0:
                return bias_first[which][:, 0, t : t + 1]
            return bias_rest[which][:, hg - 1, t : t + 1]

        w_raw, w_codes, w_plane, v_codes, x_raw, x_codes, x_plane, y_plane = {}, {}, {}, {}, {}, {}, {}, {}
        for g in range(K_PASSES):
            for hg in range(H_GROUPS):
                w_raw[g, hg] = keep.tile([P, PACK, GROUP], BF16, name="w_raw%d%d" % (g, hg), tag="w_raw%d%d" % (g, hg))
                w_codes[g, hg] = keep.tile([P, GROUP], U32, name="w_codes%d%d" % (g, hg), align_bytes=ALIGN)
                w_plane[g, hg] = keep.tile([P, GROUP], U8, name="w_plane%d%d" % (g, hg), align_bytes=ALIGN)
            for half in range(HALVES):
                v_codes[g, half] = keep.tile([P, HALF], U32, name="v_codes%d%d" % (g, half), align_bytes=ALIGN)
                x_codes[g, half] = keep.tile([P, HALF], U32, name="x_codes%d%d" % (g, half), align_bytes=ALIGN)
                x_plane[g, half] = keep.tile([P, HALF], U8, name="x_plane%d%d" % (g, half), align_bytes=ALIGN)
        for i in range(M // P):
            x_raw[i] = keep.tile([P, D], BF16, name="x_raw%d" % i)
        for hg in range(H_GROUPS):
            y_plane[hg] = keep.tile([P, M], U8, name="y_plane%d" % hg, align_bytes=ALIGN)

        def load_w(g, hg):
            rows = w1[g * GROUP : (g + 1) * GROUP, hg * GROUP : (hg + 1) * GROUP]
            nc.sync.dma_start(out=w_raw[g, hg][:], in_=rows.rearrange("(p j) c -> p j c", j=PACK))

        def load_v(g, half):
            words = v_words[g].rearrange("p n t -> p (n t)")[:, half * HALF * PACK : (half + 1) * HALF * PACK]
            nc.sync.dma_start(out=v_codes[g, half][:].bitcast(I32), in_=words.bitcast(I32))

        def load_x(pair):
            for i in (2 * pair, 2 * pair + 1):
                nc.sync.dma_start(out=x_raw[i][:], in_=x[i * P : (i + 1) * P, :])

        def load_v_scales():
            for q in range(QUADRANTS):
                nc.sync.dma_start(
                    out=v_plane[QUADRANT * q : QUADRANT * q + SCALE_ROWS, :, :].bitcast(I32),
                    in_=v_scales[:, SCALE_ROWS * q : SCALE_ROWS * (q + 1), :].rearrange("g r n -> r g n").bitcast(I32),
                )

        def load_biases(tiles, groups):
            for which, vec in enumerate((b1, db1)):
                nc.sync.dma_start(out=tiles[which][:], in_=vec.rearrange("(g p t) -> p g t", p=P, t=PACK)[:, groups])

        warm_in = keep.tile([P, PACK * P], BF16, name="warm_in", align_bytes=ALIGN)
        warm_codes = keep.tile([P, P], U32, name="warm_codes", align_bytes=ALIGN)
        warm_plane = keep.tile([P, P], U8, name="warm_plane", align_bytes=ALIGN)
        nc.vector.memset(warm_in[:], 0.0)
        nc.vector.quantize_mx(out=warm_codes[:].bitcast(E4M3X4), scales=warm_plane[:], in_=warm_in[:])
        nc.vector.memset(v_plane[:].rearrange("p g n -> p (g n)").bitcast(I32), 0)

        def warm_up():
            idle = bank(0)
            for i in range(WARM_PASSES):
                nc.tensor.matmul_mx(
                    out=idle[:, :P],
                    lhsT=warm_codes[:].bitcast(E4M3X4),
                    lhsT_scale=warm_plane[:],
                    rhs=warm_codes[:].bitcast(E4M3X4),
                    rhs_scale=warm_plane[:],
                    start=True,
                    stop=True,
                )

        make_identity(nc, ident[:])
        load_x(0)
        load_w(0, 0)
        load_x(1)
        load_v(0, 0)
        load_v_scales()
        load_w(1, 0)
        load_w(2, 0)
        load_v(1, 0)
        load_v(2, 0)
        load_biases(bias_first, slice(0, 1))
        load_x(2)
        for g in range(K_PASSES):
            load_v(g, 1)
        load_x(3)
        for g in range(K_PASSES):
            load_w(g, 1)
        load_biases(bias_rest, slice(1, H_GROUPS))
        for g in range(K_PASSES):
            load_w(g, 2)

        w_grouped, x_turned, x_grouped = {}, {}, {}

        def sort_w(g, hg, vector_runs):
            grouped = work.tile([P, PACK * GROUP], BF16, name="w_grouped", tag="w_grouped", bufs=3, align_bytes=ALIGN)
            src = w_raw[g, hg][:].rearrange("p j (c m t) -> p c t m j", m=2, t=PACK)
            dst = grouped[:].rearrange("p (t c m j) -> p c t m j", t=PACK, m=2, j=PACK)
            nc.vector.tensor_copy(out=dst[:, :vector_runs], in_=src[:, :vector_runs])
            if vector_runs < W_RUNS:
                nc.scalar.copy(out=dst[:, vector_runs:], in_=src[:, vector_runs:])
            w_grouped[g, hg] = grouped

        def quant_w(g, hg, slots=slice(0, PACK)):
            cols = slice(slots.start * P, slots.stop * P)
            nc.vector.quantize_mx(
                out=w_codes[g, hg][:, cols].bitcast(E4M3X4),
                scales=w_plane[g, hg][:, cols],
                in_=w_grouped[g, hg][:, slots.start * GROUP : slots.stop * GROUP],
            )

        def quant_w_by_halves(g):
            quant_w(g, 0, slice(0, 2))
            quant_w(g, 0, slice(2, PACK))

        def x_pairs(i):
            return x_raw[i][:].bitcast(F32).rearrange("r (g p u) -> r g u p", g=K_PASSES, u=2)

        def sort_x(pair):
            views = []
            for i in (2 * pair, 2 * pair + 1):
                ordered = work.tile([P, D // 2], F32, name="x_sorted", tag="x_sorted", bufs=4)
                nc.vector.tensor_copy(
                    out=ordered[:].rearrange("r (g u c i) -> r g c u i", g=K_PASSES, u=2, i=4),
                    in_=x_raw[i][:].bitcast(F32).rearrange("r (g c i u) -> r g c u i", g=K_PASSES, u=2, i=4),
                )
                views.append(ordered[:].rearrange("r (g u p) -> r g u p", g=K_PASSES, u=2))
            return views

        def turn_x(pair, banks, views):
            for g in range(K_PASSES):
                x_turned[pair, g] = bank(banks[g])
            for a in range(2):
                for g in range(K_PASSES):
                    for u in range(2):
                        col = (2 * a + u) * P
                        nc.tensor.transpose(x_turned[pair, g][:, col : col + P], views[a][:, g, u, :], ident[:])

        def drain_x(pair, g):
            grouped = work.tile([P, PAIR * PACK], BF16, name="x_grouped", tag="x_grouped", bufs=4, align_bytes=ALIGN)
            nc.scalar.copy(
                out=grouped[:].bitcast(F32).rearrange("p (a r u) -> p a r u", a=2, u=2),
                in_=x_turned[pair, g][:].rearrange("p (a u r) -> p a r u", a=2, u=2),
            )
            x_grouped[pair, g] = grouped

        def quant_x(pair, g):
            half, part = divmod(pair, 2)
            cols = slice(part * PAIR, (part + 1) * PAIR)
            nc.vector.quantize_mx(
                out=x_codes[g, half][:, cols].bitcast(E4M3X4),
                scales=x_plane[g, half][:, cols],
                in_=x_grouped[pair, g][:],
            )

        def z_pass(acc, hg, half, t, g):
            cols = slice(t * P, (t + 1) * P)
            nc.tensor.matmul_mx(
                out=acc[:],
                lhsT=w_codes[g, hg][:, cols].bitcast(E4M3X4),
                lhsT_scale=w_plane[g, hg][:, cols],
                rhs=x_codes[g, half][:].bitcast(E4M3X4),
                rhs_scale=x_plane[g, half][:],
                start=(g == 0),
                stop=(g == K_PASSES - 1),
            )

        def dz_pass(acc, hg, half, t, g):
            cols = slice(t * P, (t + 1) * P)
            nc.tensor.matmul_mx(
                out=acc[:],
                lhsT=w_codes[g, hg][:, cols].bitcast(E4M3X4),
                lhsT_scale=w_plane[g, hg][:, cols],
                rhs=v_codes[g, half][:].bitcast(E5M2X4),
                rhs_scale=v_plane[:, g, half * HALF : (half + 1) * HALF],
                start=(g == 0),
                stop=(g == K_PASSES - 1),
            )

        def z_group(acc, hg, half, t):
            for g in range(K_PASSES):
                z_pass(acc, hg, half, t, g)

        def dz_group(acc, hg, half, t):
            for g in range(K_PASSES):
                dz_pass(acc, hg, half, t, g)

        def slope(z, hg, t):
            s = work.tile([P, HALF], F32, name="slope", tag="slope", bufs=4)
            nc.scalar.activation(out=s[:], in_=z[:], func=SIGMOID, bias=bias_col(0, hg, t))
            return s

        def new_y():
            return work.tile([P, PACK, HALF], F32, name="y", tag="y", bufs=3, align_bytes=64)

        def tangent(y, dz, s, hg, t):
            nc.vector.scalar_tensor_tensor(
                out=y[:, t, :], in0=dz[:], scalar=bias_col(1, hg, t), in1=s[:], op0=ADD, op1=MULT
            )

        def round_y(y, vector_runs):
            y_bf = work.tile([P, HALF * PACK], BF16, name="y_bf", tag="y_bf", bufs=2, align_bytes=ALIGN)
            dst = y_bf[:].rearrange("p (c i t) -> p c t i", i=4, t=PACK)
            src = y[:].rearrange("p t (c i) -> p c t i", i=4)
            nc.vector.tensor_copy(out=dst[:, :vector_runs], in_=src[:, :vector_runs])
            if vector_runs < Y_RUNS:
                nc.scalar.copy(out=dst[:, vector_runs:], in_=src[:, vector_runs:])
            return y_bf

        def quant_y(y_bf, hg, half):
            codes = work.tile([P, HALF], U32, name="y_codes", tag="y_codes", bufs=3, align_bytes=ALIGN)
            nc.vector.quantize_mx(
                out=codes[:].bitcast(E4M3X4),
                scales=y_plane[hg][:, half * HALF : (half + 1) * HALF],
                in_=y_bf[:],
            )
            words = out_1[hg].rearrange("p m t -> p (m t)")[:, half * HALF * PACK : (half + 1) * HALF * PACK]
            nc.sync.dma_start(out=words.bitcast(I32), in_=codes[:].bitcast(I32))

        def store_y_scales(hg):
            for q in range(QUADRANTS):
                nc.sync.dma_start(
                    out=out_2[hg, SCALE_ROWS * q : SCALE_ROWS * (q + 1), :].bitcast(I32),
                    in_=y_plane[hg][QUADRANT * q : QUADRANT * q + SCALE_ROWS, :].bitcast(I32),
                )

        def turn_y(y, banks):
            turned = []
            for i in range(HALF // P):
                yt = bank(banks[i])
                for t in range(PACK):
                    nc.tensor.transpose(yt[:, t * P : (t + 1) * P], y[:, t, i * P : (i + 1) * P], ident[:])
                turned.append(yt)
            return turned

        def drain_y(yt, hg, half, i):
            rows = work.tile([P, GROUP], F32, name="y_rows", tag="y_rows", bufs=5)
            nc.scalar.copy(
                out=rows[:].rearrange("m (p t) -> m p t", t=PACK), in_=yt[:].rearrange("m (t p) -> m p t", t=PACK)
            )
            m0 = half * HALF + i * P
            nc.sync.dma_start(out=out_0[m0 : m0 + P, hg * GROUP : (hg + 1) * GROUP], in_=rows[:])

        def flip_y(y, flipped, t):
            nc.vector.transpose(out=flipped[:, t, :], in_=y[:, t, :])

        def drain_flipped(flipped, hg, half, part):
            rows = keep.tile([P, HALF // 2, PACK], F32, name="flip_rows", tag="w_raw%d0" % part)
            cols = slice(part * HALF // 2, (part + 1) * HALF // 2)
            nc.scalar.copy(out=rows[:], in_=flipped[:, :, cols].rearrange("p t n -> p n t"))
            m0 = half * HALF + part * HALF // 2
            for q in range(QUADRANTS):
                h0 = hg * GROUP + q * P
                nc.sync.dma_start(
                    out=out_0[m0 : m0 + HALF // 2, h0 : h0 + P].rearrange("(b i) h -> i b h", i=QUADRANT),
                    in_=rows[QUADRANT * q : QUADRANT * (q + 1)].rearrange("i (b j) t -> i b (j t)", j=QUADRANT),
                )

        warm_up()
        turn_x(0, (4, 5, 6), [x_pairs(0), x_pairs(1)])
        warm_up()
        for g in range(K_PASSES):
            drain_x(0, g)
        sort_w(0, 0, W_RUNS)
        quant_x(0, 0)
        quant_w_by_halves(0)
        quant_x(0, 1)
        quant_x(0, 2)
        turn_x(1, (7, 4, 5), [x_pairs(2), x_pairs(3)])
        for g in range(K_PASSES):
            drain_x(1, g)
        quant_x(1, 0)
        for g in (1, 2):
            sort_w(g, 0, W_VECTOR_RUNS)
            quant_x(1, g)
            quant_w_by_halves(g)
        dz = [bank(t) for t in range(PACK)]
        z = [bank(b) for b in (6, 7, 4, 5)]
        for product, acc, g in (
            (dz_pass, dz, 0),
            (z_pass, z, 0),
            (z_pass, z, 1),
            (dz_pass, dz, 1),
            (z_pass, z, 2),
            (dz_pass, dz, 2),
        ):
            for t in range(PACK):
                product(acc[t], 0, 0, t, g)
        views = sort_x(2)
        y_first = new_y()
        for t in range(PACK):
            tangent(y_first, dz[t], slope(z[t], 0, t), 0, t)

        turn_x(2, (6, 7, 4), views)
        for g in range(K_PASSES):
            drain_x(2, g)
        views = sort_x(3)
        for g in range(K_PASSES):
            quant_x(2, g)
        dz = [bank(t) for t in range(PACK)]
        dz_group(dz[0], 0, 1, 0)
        dz_group(dz[1], 0, 1, 1)
        sort_w(0, 1, W_VECTOR_RUNS)
        turn_x(3, (5, 6, 7), views)
        for g in range(K_PASSES):
            drain_x(3, g)
            quant_x(3, g)
            if g == 0:
                quant_w(0, 1)
        sort_w(1, 1, W_VECTOR_RUNS)
        dz_group(dz[2], 0, 1, 2)
        dz_group(dz[3], 0, 1, 3)
        turned = turn_y(y_first, HIGH_BANKS)
        for i in range(HALF // P):
            drain_y(turned[i], 0, 0, i)
        sort_w(2, 1, W_VECTOR_RUNS)
        quant_w(1, 1)
        quant_w(2, 1)
        y_last = new_y()
        for t in range(PACK):
            z_slot = bank(HIGH_BANKS[t])
            z_group(z_slot, 0, 1, t)
            tangent(y_last, dz[t], slope(z_slot, 0, t), 0, t)

        units = [(1, 1), (1, 0), (2, 0), (2, 1)]
        flipped_unit = (1, 0)
        last = (0, 1)
        flipped_last = None
        owed = [(y_first, 0, 0), (y_last, 0, 1)]
        rounded = []
        halves_done = [0] * H_GROUPS
        to_sort = list(range(K_PASSES))
        to_quantise = []
        for n, (hg, half) in enumerate(units):
            y = new_y()
            flipped = None
            if (hg, half) == flipped_unit:
                flipped = work.tile([P, PACK, HALF], F32, name="flipped", tag="flipped", bufs=1, align_bytes=64)
            for t in range(PACK):
                first_bank = LOW_PAIRS[(t + n) % 2]
                if t == 3:
                    first_bank = HIGH_BANKS[0]
                if t == 2 and flipped_last is not None:
                    first_bank = HIGH_BANKS[2]
                z_slot = bank(first_bank)
                dz_slot = bank(first_bank + 1)
                z_group(z_slot, hg, half, t)
                dz_group(dz_slot, hg, half, t)
                s = slope(z_slot, hg, t)
                if flipped_last is None:
                    if t == 1:
                        turned = turn_y(y_last, HIGH_BANKS)
                        drain_y(turned[0], last[0], last[1], 0)
                    if t >= 1:
                        drain_y(turned[t], last[0], last[1], t)
                elif t >= 2:
                    drain_flipped(flipped_last, last[0], last[1], t - 2)
                tangent(y, dz_slot, s, hg, t)
                if rounded:
                    y_bf, hg_owed, half_owed = rounded.pop()
                    quant_y(y_bf, hg_owed, half_owed)
                    halves_done[hg_owed] += 1
                    if halves_done[hg_owed] == HALVES:
                        store_y_scales(hg_owed)
                if t == 0:
                    y_owed, hg_owed, half_owed = owed.pop(0)
                    rounded.append((round_y(y_owed, Y_RUNS // 2), hg_owed, half_owed))
                if t == 2 and flipped_last is not None:
                    y_owed, hg_owed, half_owed = owed.pop(0)
                    rounded.append((round_y(y_owed, Y_RUNS), hg_owed, half_owed))
                if to_quantise:
                    quant_w(to_quantise.pop(), 2)
                if t in (1, 2) and to_sort:
                    g = to_sort.pop(0)
                    sort_w(g, 2, W_VECTOR_RUNS)
                    to_quantise.append(g)
                if flipped is not None and t > 0:
                    flip_y(y, flipped, t - 1)
                if flipped_last is not None and t == 0:
                    flip_y(y_last, flipped_last, PACK - 1)
            flipped_last = flipped
            y_last, last = y, (hg, half)
            owed.append((y, hg, half))

        turned = turn_y(y_last, (0, 1, 6, 7))
        y_bf = round_y(y_last, Y_RUNS)
        for i in range(HALF // P - 1):
            drain_y(turned[i], last[0], last[1], i)
        quant_y(y_bf, last[0], last[1])
        drain_y(turned[-1], last[0], last[1], HALF // P - 1)
        store_y_scales(last[0])
